import numpy as np
import ml_dtypes


def mxq(x, axis, fmt="e4m3"):
    dtype, down = {"e4m3": (ml_dtypes.float8_e4m3fn, 7), "e5m2": (ml_dtypes.float8_e5m2, 14)}[fmt]
    v = np.moveaxis(np.asarray(x, np.float32).astype(ml_dtypes.bfloat16).astype(np.float64), axis, -1)
    blocks = v.reshape(v.shape[:-1] + (-1, 32))
    amax = np.abs(blocks).max(-1, keepdims=True)
    byte = np.maximum(np.where(amax > 0, np.frexp(amax)[1] - 1 + 127, 0) - down, 1)
    scale = np.exp2(byte - 127.0)
    codes = (blocks / scale).astype(np.float32).astype(dtype).astype(np.float64)
    return np.moveaxis((codes * scale).reshape(v.shape), -1, axis)


WIDE = False


def mx_kscale(k):
    if not WIDE:
        return np.ones(k)
    levels = np.array([10, -10, 5, -5, 0])
    if k % 512:
        return np.exp2(np.random.permutation(np.resize(levels, k // 32))).repeat(32)
    a = np.empty((k // 512, 16))
    for p in range(k // 512):
        a[p, :8] = np.random.permutation(np.resize(levels, 8))
        for g in range(8):
            far = levels[np.abs(levels - a[p, g]) >= 10]
            a[p, g + 8] = far[np.random.randint(len(far))]
    return np.exp2(a.ravel()).repeat(32)


def f64(x):
    return np.asarray(x).astype(np.float64)


def striped(idx):
    return np.tile(idx.reshape(-1, 16).T, (8, 1)).astype(np.uint16)


def unstriped(offs):
    return offs[:16].T.reshape(-1).astype(np.int64)


def pack_weight(w):
    k, n = w.shape
    w = f64(np.asarray(w, np.float32).astype(ml_dtypes.bfloat16)).reshape(k // 32, 32, n)
    amax = np.abs(w).max(1)
    byte = np.clip(np.where(amax > 0, np.frexp(amax)[1] - 1 + 127 - 7, 1), 1, 254)
    scaled = (w * np.exp2(127.0 - byte)[:, None, :]).reshape(k, n).astype(np.float32)
    words = np.ascontiguousarray(scaled.reshape(k // 512, 128, 4, n).transpose(0, 1, 3, 2)).astype(ml_dtypes.float8_e4m3fn).view(np.uint8)
    return words, np.ascontiguousarray(byte.astype(np.uint8).reshape(k // 512, 16, n))


def unpack_weight(words, scales):
    g, p, n, _ = words.shape
    vals = np.ascontiguousarray(words).view(ml_dtypes.float8_e4m3fn).astype(np.float64) * np.repeat(np.exp2(scales.astype(np.float64) - 127.0), 8, axis=1)[..., None]
    return vals.transpose(0, 1, 3, 2).reshape(g * 512, n)


def planes(y):
    n, m = y.shape
    v = y.astype(np.float32).astype(ml_dtypes.bfloat16).astype(np.float64).reshape(n // 32, 32, m)
    top = np.abs(v).max(1)
    byte = np.clip(np.where(top > 0, np.frexp(top)[1] - 1 + 127 - 7, 1), 1, 254)
    codes = (v * np.exp2(127.0 - byte)[:, None, :]).reshape(n, m).astype(np.float32).astype(ml_dtypes.float8_e4m3fn).view(np.uint8)
    words = codes.reshape(n // 512, 128, 4, m).transpose(0, 1, 3, 2)
    return np.ascontiguousarray(words), np.ascontiguousarray(byte.astype(np.uint8).reshape(n // 512, 16, m))


def relu(v):
    return np.maximum(v, 0.0)


K, T, S, H, N, V = 512, 2048, 512, 512, 512, 256


def setup_inputs():
    n = np.random.standard_normal
    s = mx_kscale(K)[:, None]
    u = mx_kscale(H)
    packed_xT = pack_weight(n((K, T)) * s)
    return {
        "x_words": packed_xT[0],
        "x_scales": packed_xT[1],
        "w1": (n((K, H)) / np.sqrt(K) / s * u).astype(np.float32),
        "w2": (n((H, N)) / np.sqrt(H) / u[:, None]).astype(np.float32),
        "meas": (n((N, V))).astype(np.float32),
        "offs": striped(np.random.permutation(T)[:S]),
        "line": striped(np.random.permutation(S)[:V]),
    }


def reference(x_words, x_scales, w1, w2, meas, offs, line):
    xq = unpack_weight(x_words, x_scales)[:, unstriped(offs)]
    h = relu(mxq(f64(w1), 0, "e4m3").T @ xq)
    y = mxq(f64(w2), 0, "e4m3").T @ mxq(h, 0, "e4m3")
    out = y.copy()
    out[:, unstriped(line)] = 0.25 * y[:, unstriped(line)] + 0.75 * f64(meas)
    out_0 = out
    return (out_0,) + planes(out_0)

@@ -1,0 +1,183 @@
+from contextlib import ExitStack
+
+import concourse.mybir as mybir
+
+K, T, S, H, N, V = 512, 2048, 512, 512, 512, 256
+FLOPS = 2 * K * H * S + 2 * H * N * S
+
+F32 = mybir.dt.float32
+BF16 = mybir.dt.bfloat16
+I32 = mybir.dt.int32
+U32 = mybir.dt.uint32
+U16 = mybir.dt.uint16
+U8 = mybir.dt.uint8
+FP8X4 = mybir.dt.float8_e4m3fn_x4
+ALU = mybir.AluOpType
+ACT = mybir.ActivationFunctionType
+
+P = 128
+PACK = 4
+CHUNK = 128
+W1_VECTOR_M = 84
+W2_VECTOR_M = 84
+LAST_VECTOR_COLS = 384
+
+
+def tile_picked_ydcons_relu_po_kernel(
+    tc, x_words, x_scales, w1, w2, meas, offs, line, out_0, out_1, out_2
+):
+    nc = tc.nc
+    with ExitStack() as ctx:
+        lists = ctx.enter_context(tc.tile_pool(name="lists", bufs=1))
+        sb = ctx.enter_context(tc.tile_pool(name="sb", bufs=1))
+        ps = ctx.enter_context(tc.psum_pool(name="ps", bufs=1))
+
+        offs_sb = lists.tile([P, S // 16], U16, name="offs_sb")
+        line_sb = lists.tile([P, V // 16], U16, name="line_sb")
+
+        def sbuf(shape, dtype, name):
+            return sb.tile(shape, dtype, name=name, align_bytes=64)
+
+        x_scale_table = sbuf([P, T], U8, "x_scale_table")
+        nc.vector.memset(x_scale_table[:].bitcast(I32), 0)
+        quarter = sbuf([P, V], F32, "quarter")
+        nc.gpsimd.memset(quarter[:], 0.25)
+
+        nc.sync.dma_start(offs_sb[:], offs)
+        nc.sync.dma_start(line_sb[:], line)
+        w1_raw = sbuf([P, PACK, H], F32, "w1_raw")
+        nc.sync.dma_start(w1_raw[:], w1.rearrange("(p j) c -> p j c", j=PACK))
+        for q in range(4):
+            nc.sync.dma_start(
+                x_scale_table[32 * q : 32 * q + 4, :].bitcast(I32),
+                x_scales[0, 4 * q : 4 * q + 4, :].bitcast(I32),
+            )
+        x_word_table = sbuf([P, T], U32, "x_word_table")
+        nc.sync.dma_start(
+            x_word_table[:].bitcast(I32), x_words[0].rearrange("p n t -> p (n t)").bitcast(I32)
+        )
+        w2_raw = sbuf([P, PACK, N], F32, "w2_raw")
+        nc.sync.dma_start(w2_raw[:], w2.rearrange("(p j) c -> p j c", j=PACK))
+        meas_raw = sbuf([P, PACK, V], F32, "meas_raw")
+        nc.sync.dma_start(meas_raw[:], meas.rearrange("(p t) v -> p t v", t=PACK))
+
+        def deal(raw, name, vector_m, t_lo, t_hi):
+            nt = t_hi - t_lo
+            dealt = sbuf([P, nt * P * PACK], BF16, name + "_bf16")
+            dst = dealt[:].rearrange("p (t m j) -> p m t j", t=nt, j=PACK)
+            src = raw[:].rearrange("p j (m t) -> p m t j", t=PACK)[:, :, t_lo:t_hi, :]
+            if vector_m > 0:
+                nc.vector.tensor_copy(dst[:, :vector_m], src[:, :vector_m])
+            nc.scalar.copy(dst[:, vector_m:], src[:, vector_m:])
+            return dealt
+
+        def quantize(values, name):
+            width = values.shape[1] // PACK
+            codes = sbuf([P, width], U32, name + "_codes")
+            scales = sbuf([P, width], U8, name + "_scales")
+            nc.vector.quantize_mx(out=codes[:].bitcast(FP8X4), scales=scales[:], in_=values)
+            return codes, scales
+
+        x_scales_picked = sbuf([P, S], U8, "x_scales_picked")
+        nc.vector.tensor_copy(x_scales_picked[:], x_scale_table[:].indirect(offs_sb[:]))
+
+        w1_codes, w1_scales = quantize(deal(w1_raw, "w1", W1_VECTOR_M, 0, PACK)[:], "w1")
+
+        half = S // 2
+        x_picked = []
+        for u in range(2):
+            words = sbuf([P, half], U32, "x_picked%d" % u)
+            nc.vector.tensor_copy(
+                words[:], x_word_table[:].indirect(offs_sb[:, u * half // 16 : (u + 1) * half // 16])
+            )
+            x_picked.append(words)
+
+        n_chunks = S // CHUNK
+        h_banks = []
+        for c in range(n_chunks):
+            bank = ps.tile([P, PACK, CHUNK], F32, name="h_bank%d" % c)
+            u, lo = divmod(c * CHUNK, half)
+            for t in range(PACK):
+                cols = slice(t * P, (t + 1) * P)
+                nc.tensor.matmul_mx(
+                    out=bank[:, t, :],
+                    lhsT=w1_codes[:, cols].bitcast(FP8X4),
+                    lhsT_scale=w1_scales[:, cols],
+                    rhs=x_picked[u][:, lo : lo + CHUNK].bitcast(FP8X4),
+                    rhs_scale=x_scales_picked[:, c * CHUNK : (c + 1) * CHUNK],
+                    start=True,
+                    stop=True,
+                )
+            h_banks.append(bank)
+
+        h_q = []
+        w2_q = []
+        for c in range(n_chunks):
+            h_bf16 = sbuf([P, CHUNK * PACK], BF16, "h_bf16_%d" % c)
+            dst = h_bf16[:].rearrange("p (n t) -> p n t", t=PACK)
+            src = h_banks[c][:].rearrange("p t n -> p n t")
+            if c % 2 == 0:
+                nc.vector.tensor_scalar_max(dst, src, 0.0)
+            else:
+                nc.scalar.activation(dst, src, ACT.Relu)
+            h_q.append(quantize(h_bf16[:], "h%d" % c))
+            if c == 1:
+                w2_q.append(quantize(deal(w2_raw, "w2a", W2_VECTOR_M, 0, 2)[:], "w2a"))
+        w2_q.append(quantize(deal(w2_raw, "w2b", 0, 2, 4)[:], "w2b"))
+
+        meas_part = sbuf([P, PACK, V], F32, "meas_part")
+        out_bf16 = sbuf([P, S, PACK], BF16, "out_bf16")
+        out_rows = out_0.rearrange("(p t) n -> p t n", t=PACK)
+        y_tiles = []
+        for t in range(PACK):
+            bank = ps.tile([P, S], F32, name="y_bank%d" % t)
+            w2_codes, w2_scales = w2_q[t // 2]
+            cols = slice((t % 2) * P, (t % 2 + 1) * P)
+            for c in range(n_chunks):
+                h_codes, h_scales = h_q[c]
+                nc.tensor.matmul_mx(
+                    out=bank[:, c * CHUNK : (c + 1) * CHUNK],
+                    lhsT=w2_codes[:, cols].bitcast(FP8X4),
+                    lhsT_scale=w2_scales[:, cols],
+                    rhs=h_codes[:].bitcast(FP8X4),
+                    rhs_scale=h_scales[:],
+                    start=True,
+                    stop=True,
+                )
+            y = sbuf([P, S], F32, "y%d" % t)
+            nc.scalar.copy(y[:], bank[:])
+            nc.scalar.mul(meas_part[:, t, :], meas_raw[:, t, :], 0.75)
+            y_tiles.append(y)
+
+        for t in range(PACK):
+            y = y_tiles[t]
+            picked = sbuf([P, V], F32, "picked%d" % t)
+            nc.vector.tensor_tensor(picked[:], y[:].indirect(line_sb[:]), quarter[:], ALU.mult)
+            nc.vector.tensor_tensor(y[:].indirect(line_sb[:]), picked[:], meas_part[:, t, :], ALU.add)
+            nc.sync.dma_start(out_rows[:, t, :], y[:])
+            if t < PACK - 2:
+                nc.scalar.copy(out_bf16[:, :, t], y[:])
+            elif t == PACK - 2:
+                nc.scalar.copy(out_bf16[:, :, t:], y[:].unsqueeze(2).to_broadcast([P, S, 2]))
+            else:
+                nc.vector.tensor_copy(out_bf16[:, :half, t], y[:, :half])
+                nc.vector.tensor_copy(out_bf16[:, half:LAST_VECTOR_COLS, t], y[:, half:LAST_VECTOR_COLS])
+                nc.scalar.copy(out_bf16[:, LAST_VECTOR_COLS:, t], y[:, LAST_VECTOR_COLS:])
+
+        out_codes = sbuf([P, S], U32, "out_codes")
+        out_scales = sbuf([P, S], U8, "out_scales")
+        out_words = out_1[0].rearrange("p n t -> p (n t)").bitcast(I32)
+        for u in range(2):
+            cols = slice(u * half, (u + 1) * half)
+            nc.vector.quantize_mx(
+                out=out_codes[:, cols].bitcast(FP8X4),
+                scales=out_scales[:, cols],
+                in_=out_bf16[:, cols, :].rearrange("p n t -> p (n t)"),
+            )
+            nc.sync.dma_start(out_words[:, cols], out_codes[:, cols].bitcast(I32))
+        for q in range(4):
+            queue = nc.scalar if q % 2 == 0 else nc.sync
+            queue.dma_start(
+                out_2[0, 4 * q : 4 * q + 4, :].bitcast(I32),
+                out_scales[32 * q : 32 * q + 4, :].bitcast(I32),
+            )

@@ -19,7 +19,8 @@ P = 128
 PACK = 4
 CHUNK = 128
 W1_VECTOR_M = 84
-W2_VECTOR_M = 84
+W2A_VECTOR_M = 52
+W2B_VECTOR_M = 96
 LAST_VECTOR_COLS = 384
 
 
@@ -35,18 +36,18 @@ def tile_picked_ydcons_relu_po_kernel(
         offs_sb = lists.tile([P, S // 16], U16, name="offs_sb")
         line_sb = lists.tile([P, V // 16], U16, name="line_sb")
 
-        def sbuf(shape, dtype, name):
-            return sb.tile(shape, dtype, name=name, align_bytes=64)
+        def sbuf(shape, dtype, name, tag=None):
+            return sb.tile(shape, dtype, name=name, tag=tag or name, align_bytes=64)
 
         x_scale_table = sbuf([P, T], U8, "x_scale_table")
         nc.vector.memset(x_scale_table[:].bitcast(I32), 0)
         quarter = sbuf([P, V], F32, "quarter")
-        nc.gpsimd.memset(quarter[:], 0.25)
+        nc.vector.memset(quarter[:], 0.25)
 
-        nc.sync.dma_start(offs_sb[:], offs)
-        nc.sync.dma_start(line_sb[:], line)
         w1_raw = sbuf([P, PACK, H], F32, "w1_raw")
         nc.sync.dma_start(w1_raw[:], w1.rearrange("(p j) c -> p j c", j=PACK))
+        nc.sync.dma_start(offs_sb[:], offs)
+        nc.sync.dma_start(line_sb[:], line)
         for q in range(4):
             nc.sync.dma_start(
                 x_scale_table[32 * q : 32 * q + 4, :].bitcast(I32),
@@ -56,20 +57,21 @@ def tile_picked_ydcons_relu_po_kernel(
         nc.sync.dma_start(
             x_word_table[:].bitcast(I32), x_words[0].rearrange("p n t -> p (n t)").bitcast(I32)
         )
-        w2_raw = sbuf([P, PACK, N], F32, "w2_raw")
-        nc.sync.dma_start(w2_raw[:], w2.rearrange("(p j) c -> p j c", j=PACK))
+        w2_rows = w2.rearrange("(p j) c -> p j c", j=PACK)
+        w2_raw = []
+        for u in range(2):
+            part = sbuf([P, PACK, N // 2], F32, "w2_raw%d" % u)
+            nc.sync.dma_start(part[:], w2_rows[:, :, u * N // 2 : (u + 1) * N // 2])
+            w2_raw.append(part)
         meas_raw = sbuf([P, PACK, V], F32, "meas_raw")
         nc.sync.dma_start(meas_raw[:], meas.rearrange("(p t) v -> p t v", t=PACK))
 
-        def deal(raw, name, vector_m, t_lo, t_hi):
+        def deal_views(raw, name, t_lo, t_hi, tag=None):
             nt = t_hi - t_lo
-            dealt = sbuf([P, nt * P * PACK], BF16, name + "_bf16")
+            dealt = sbuf([P, nt * P * PACK], BF16, name + "_bf16", tag)
             dst = dealt[:].rearrange("p (t m j) -> p m t j", t=nt, j=PACK)
             src = raw[:].rearrange("p j (m t) -> p m t j", t=PACK)[:, :, t_lo:t_hi, :]
-            if vector_m > 0:
-                nc.vector.tensor_copy(dst[:, :vector_m], src[:, :vector_m])
-            nc.scalar.copy(dst[:, vector_m:], src[:, vector_m:])
-            return dealt
+            return dealt, dst, src
 
         def quantize(values, name):
             width = values.shape[1] // PACK
@@ -78,10 +80,23 @@ def tile_picked_ydcons_relu_po_kernel(
             nc.vector.quantize_mx(out=codes[:].bitcast(FP8X4), scales=scales[:], in_=values)
             return codes, scales
 
+        def product(out, weights, w_cols, moving_codes, moving_scales):
+            nc.tensor.matmul_mx(
+                out=out,
+                lhsT=weights[0][:, w_cols].bitcast(FP8X4),
+                lhsT_scale=weights[1][:, w_cols],
+                rhs=moving_codes.bitcast(FP8X4),
+                rhs_scale=moving_scales,
+                start=True,
+                stop=True,
+            )
+
+        w1_bf16, dst, src = deal_views(w1_raw, "w1", 0, PACK)
+        nc.vector.tensor_copy(dst[:, :W1_VECTOR_M], src[:, :W1_VECTOR_M])
+        nc.scalar.copy(dst[:, W1_VECTOR_M:], src[:, W1_VECTOR_M:])
         x_scales_picked = sbuf([P, S], U8, "x_scales_picked")
         nc.vector.tensor_copy(x_scales_picked[:], x_scale_table[:].indirect(offs_sb[:]))
-
-        w1_codes, w1_scales = quantize(deal(w1_raw, "w1", W1_VECTOR_M, 0, PACK)[:], "w1")
+        w1_q = quantize(w1_bf16[:], "w1")
 
         half = S // 2
         x_picked = []
@@ -98,71 +113,87 @@ def tile_picked_ydcons_relu_po_kernel(
             bank = ps.tile([P, PACK, CHUNK], F32, name="h_bank%d" % c)
             u, lo = divmod(c * CHUNK, half)
             for t in range(PACK):
-                cols = slice(t * P, (t + 1) * P)
-                nc.tensor.matmul_mx(
-                    out=bank[:, t, :],
-                    lhsT=w1_codes[:, cols].bitcast(FP8X4),
-                    lhsT_scale=w1_scales[:, cols],
-                    rhs=x_picked[u][:, lo : lo + CHUNK].bitcast(FP8X4),
-                    rhs_scale=x_scales_picked[:, c * CHUNK : (c + 1) * CHUNK],
-                    start=True,
-                    stop=True,
+                product(
+                    bank[:, t, :],
+                    w1_q,
+                    slice(t * P, (t + 1) * P),
+                    x_picked[u][:, lo : lo + CHUNK],
+                    x_scales_picked[:, c * CHUNK : (c + 1) * CHUNK],
                 )
             h_banks.append(bank)
 
-        h_q = []
-        w2_q = []
-        for c in range(n_chunks):
-            h_bf16 = sbuf([P, CHUNK * PACK], BF16, "h_bf16_%d" % c)
+        def relu_out(c):
+            h_bf16 = sbuf([P, CHUNK * PACK], BF16, "h_bf16_%d" % c, "w2_raw1" if c == n_chunks - 1 else None)
             dst = h_bf16[:].rearrange("p (n t) -> p n t", t=PACK)
             src = h_banks[c][:].rearrange("p t n -> p n t")
-            if c % 2 == 0:
+            if c < n_chunks - 1:
                 nc.vector.tensor_scalar_max(dst, src, 0.0)
             else:
                 nc.scalar.activation(dst, src, ACT.Relu)
-            h_q.append(quantize(h_bf16[:], "h%d" % c))
-            if c == 1:
-                w2_q.append(quantize(deal(w2_raw, "w2a", W2_VECTOR_M, 0, 2)[:], "w2a"))
-        w2_q.append(quantize(deal(w2_raw, "w2b", 0, 2, 4)[:], "w2b"))
+            return h_bf16
 
-        meas_part = sbuf([P, PACK, V], F32, "meas_part")
+        w2_bf16 = sbuf([P, N * PACK], BF16, "w2_bf16")
+        w2_dealt = w2_bf16[:].rearrange("p (t m j) -> p m t j", t=PACK, j=PACK)
+        for u in range(2):
+            nc.scalar.copy(
+                w2_dealt[:, u * P // 2 : (u + 1) * P // 2],
+                w2_raw[u][:].rearrange("p j (m t) -> p m t j", t=PACK),
+            )
+        h_bf16 = [relu_out(c) for c in range(n_chunks)]
+        h_q = [quantize(h_bf16[c][:], "h%d" % c) for c in range(n_chunks - 1)]
+        w2_q0 = quantize(w2_bf16[:, : P * PACK], "w2t0")
+        h_q.append(quantize(h_bf16[n_chunks - 1][:], "h3"))
+        w2_q1 = quantize(w2_bf16[:, P * PACK : 2 * P * PACK], "w2t1")
+        w2_qb = quantize(w2_bf16[:, 2 * P * PACK :], "w2b")
+
         out_bf16 = sbuf([P, S, PACK], BF16, "out_bf16")
         out_rows = out_0.rearrange("(p t) n -> p t n", t=PACK)
         y_tiles = []
-        for t in range(PACK):
-            bank = ps.tile([P, S], F32, name="y_bank%d" % t)
-            w2_codes, w2_scales = w2_q[t // 2]
-            cols = slice((t % 2) * P, (t % 2 + 1) * P)
-            for c in range(n_chunks):
-                h_codes, h_scales = h_q[c]
-                nc.tensor.matmul_mx(
-                    out=bank[:, c * CHUNK : (c + 1) * CHUNK],
-                    lhsT=w2_codes[:, cols].bitcast(FP8X4),
-                    lhsT_scale=w2_scales[:, cols],
-                    rhs=h_codes[:].bitcast(FP8X4),
-                    rhs_scale=h_scales[:],
-                    start=True,
-                    stop=True,
-                )
+
+        def second_layer(t, weights, w_cols):
             y = sbuf([P, S], F32, "y%d" % t)
-            nc.scalar.copy(y[:], bank[:])
-            nc.scalar.mul(meas_part[:, t, :], meas_raw[:, t, :], 0.75)
+            bank = ps.tile([P, S], F32, name="y_bank%d" % t)
+            pieces = [(bank, 0, n_chunks)]
+            if t == 0:
+                late = ps.tile([P, S], F32, name="y_late", tag="h_bank0")
+                pieces = [(bank, 0, n_chunks // 2), (late, n_chunks // 2, n_chunks)]
+            for piece, lo, hi in pieces:
+                for c in range(lo, hi):
+                    product(piece[:, c * CHUNK : (c + 1) * CHUNK], weights, w_cols, h_q[c][0][:], h_q[c][1][:])
+                nc.scalar.copy(y[:, lo * CHUNK : hi * CHUNK], piece[:, lo * CHUNK : hi * CHUNK])
             y_tiles.append(y)
 
-        for t in range(PACK):
-            y = y_tiles[t]
-            picked = sbuf([P, V], F32, "picked%d" % t)
-            nc.vector.tensor_tensor(picked[:], y[:].indirect(line_sb[:]), quarter[:], ALU.mult)
-            nc.vector.tensor_tensor(y[:].indirect(line_sb[:]), picked[:], meas_part[:, t, :], ALU.add)
-            nc.sync.dma_start(out_rows[:, t, :], y[:])
-            if t < PACK - 2:
-                nc.scalar.copy(out_bf16[:, :, t], y[:])
-            elif t == PACK - 2:
-                nc.scalar.copy(out_bf16[:, :, t:], y[:].unsqueeze(2).to_broadcast([P, S, 2]))
-            else:
-                nc.vector.tensor_copy(out_bf16[:, :half, t], y[:, :half])
-                nc.vector.tensor_copy(out_bf16[:, half:LAST_VECTOR_COLS, t], y[:, half:LAST_VECTOR_COLS])
-                nc.scalar.copy(out_bf16[:, LAST_VECTOR_COLS:, t], y[:, LAST_VECTOR_COLS:])
+        meas_part = [None] * PACK
+
+        def weigh_meas(t, tag=None):
+            meas_part[t] = sbuf([P, V], F32, "meas_part%d" % t, tag)
+            nc.scalar.mul(meas_part[t][:], meas_raw[:, t, :], 0.75)
+
+        second_layer(0, w2_q0, slice(0, P))
+        second_layer(1, w2_q1, slice(0, P))
+        weigh_meas(0, "w2t1_codes")
+        weigh_meas(1)
+        second_layer(2, w2_qb, slice(0, P))
+        second_layer(3, w2_qb, slice(P, 2 * P))
+        weigh_meas(2, "w2b_codes")
+        weigh_meas(3)
+
+        picked = [sbuf([P, V], F32, "picked%d" % t) for t in range(PACK)]
+        for pair in range(0, PACK, 2):
+            for t in (pair, pair + 1):
+                nc.vector.tensor_tensor(picked[t][:], y_tiles[t][:].indirect(line_sb[:]), quarter[:], ALU.mult)
+            for t in (pair, pair + 1):
+                y = y_tiles[t]
+                nc.vector.tensor_tensor(y[:].indirect(line_sb[:]), picked[t][:], meas_part[t][:], ALU.add)
+                nc.sync.dma_start(out_rows[:, t, :], y[:])
+                if t < PACK - 2:
+                    nc.scalar.copy(out_bf16[:, :, t], y[:])
+                elif t == PACK - 2:
+                    nc.scalar.copy(out_bf16[:, :, t:], y[:].unsqueeze(2).to_broadcast([P, S, 2]))
+                else:
+                    nc.vector.tensor_copy(out_bf16[:, :half, t], y[:, :half])
+                    nc.vector.tensor_copy(out_bf16[:, half:LAST_VECTOR_COLS, t], y[:, half:LAST_VECTOR_COLS])
+                    nc.scalar.copy(out_bf16[:, LAST_VECTOR_COLS:, t], y[:, LAST_VECTOR_COLS:])
 
         out_codes = sbuf([P, S], U32, "out_codes")
         out_scales = sbuf([P, S], U8, "out_scales")

@@ -18,7 +18,7 @@ ACT = mybir.ActivationFunctionType
 P = 128
 PACK = 4
 CHUNK = 128
-W1_VECTOR_M = 84
+W1_VECTOR_M = 52
 W2A_VECTOR_M = 52
 W2B_VECTOR_M = 96
 LAST_VECTOR_COLS = 384
@@ -44,10 +44,9 @@ def tile_picked_ydcons_relu_po_kernel(
         quarter = sbuf([P, V], F32, "quarter")
         nc.vector.memset(quarter[:], 0.25)
 
+        nc.sync.dma_start(offs_sb[:], offs)
         w1_raw = sbuf([P, PACK, H], F32, "w1_raw")
         nc.sync.dma_start(w1_raw[:], w1.rearrange("(p j) c -> p j c", j=PACK))
-        nc.sync.dma_start(offs_sb[:], offs)
-        nc.sync.dma_start(line_sb[:], line)
         for q in range(4):
             nc.sync.dma_start(
                 x_scale_table[32 * q : 32 * q + 4, :].bitcast(I32),
@@ -63,14 +62,15 @@ def tile_picked_ydcons_relu_po_kernel(
             part = sbuf([P, PACK, N // 2], F32, "w2_raw%d" % u)
             nc.sync.dma_start(part[:], w2_rows[:, :, u * N // 2 : (u + 1) * N // 2])
             w2_raw.append(part)
+        nc.sync.dma_start(line_sb[:], line)
         meas_raw = sbuf([P, PACK, V], F32, "meas_raw")
         nc.sync.dma_start(meas_raw[:], meas.rearrange("(p t) v -> p t v", t=PACK))
 
         def deal_views(raw, name, t_lo, t_hi, tag=None):
             nt = t_hi - t_lo
             dealt = sbuf([P, nt * P * PACK], BF16, name + "_bf16", tag)
-            dst = dealt[:].rearrange("p (t m j) -> p m t j", t=nt, j=PACK)
-            src = raw[:].rearrange("p j (m t) -> p m t j", t=PACK)[:, :, t_lo:t_hi, :]
+            dst = dealt[:].rearrange("p (t m j) -> p m j t", t=nt, j=PACK)
+            src = raw[:].rearrange("p j (m t) -> p m j t", t=PACK)[:, :, :, t_lo:t_hi]
             return dealt, dst, src
 
         def quantize(values, name):
@@ -133,11 +133,11 @@ def tile_picked_ydcons_relu_po_kernel(
             return h_bf16
 
         w2_bf16 = sbuf([P, N * PACK], BF16, "w2_bf16")
-        w2_dealt = w2_bf16[:].rearrange("p (t m j) -> p m t j", t=PACK, j=PACK)
+        w2_dealt = w2_bf16[:].rearrange("p (t m j) -> p m j t", t=PACK, j=PACK)
         for u in range(2):
             nc.scalar.copy(
                 w2_dealt[:, u * P // 2 : (u + 1) * P // 2],
-                w2_raw[u][:].rearrange("p j (m t) -> p m t j", t=PACK),
+                w2_raw[u][:].rearrange("p j (m t) -> p m j t", t=PACK),
             )
         h_bf16 = [relu_out(c) for c in range(n_chunks)]
         h_q = [quantize(h_bf16[c][:], "h%d" % c) for c in range(n_chunks - 1)]
@@ -155,8 +155,8 @@ def tile_picked_ydcons_relu_po_kernel(
             bank = ps.tile([P, S], F32, name="y_bank%d" % t)
             pieces = [(bank, 0, n_chunks)]
             if t == 0:
-                late = ps.tile([P, S], F32, name="y_late", tag="h_bank0")
-                pieces = [(bank, 0, n_chunks // 2), (late, n_chunks // 2, n_chunks)]
+                late = [ps.tile([P, S], F32, name="y_late%d" % i, tag="h_bank%d" % i) for i in range(2)]
+                pieces = [(bank, 0, 2), (late[0], 2, 3), (late[1], 3, 4)]
             for piece, lo, hi in pieces:
                 for c in range(lo, hi):
                     product(piece[:, c * CHUNK : (c + 1) * CHUNK], weights, w_cols, h_q[c][0][:], h_q[c][1][:])
@@ -172,11 +172,11 @@ def tile_picked_ydcons_relu_po_kernel(
         second_layer(0, w2_q0, slice(0, P))
         second_layer(1, w2_q1, slice(0, P))
         weigh_meas(0, "w2t1_codes")
-        weigh_meas(1)
+        weigh_meas(1, "w2t0_codes")
         second_layer(2, w2_qb, slice(0, P))
         second_layer(3, w2_qb, slice(P, 2 * P))
         weigh_meas(2, "w2b_codes")
-        weigh_meas(3)
+        weigh_meas(3, "w2b_scales")
 
         picked = [sbuf([P, V], F32, "picked%d" % t) for t in range(PACK)]
         for pair in range(0, PACK, 2):

@@ -98,6 +98,10 @@ def tile_picked_ydcons_relu_po_kernel(
         nc.vector.tensor_copy(x_scales_picked[:], x_scale_table[:].indirect(offs_sb[:]))
         w1_q = quantize(w1_bf16[:], "w1")
 
+        warm = ps.tile([P, S], F32, name="warm", tag="y_bank3")
+        for i in range(2):
+            product(warm[:], w1_q, slice(i * P, (i + 1) * P), w1_q[0][:], w1_q[1][:])
+
         half = S // 2
         x_picked = []
         for u in range(2):
@@ -152,7 +156,7 @@ def tile_picked_ydcons_relu_po_kernel(
 
         def second_layer(t, weights, w_cols):
             y = sbuf([P, S], F32, "y%d" % t)
-            bank = ps.tile([P, S], F32, name="y_bank%d" % t)
+            bank = ps.tile([P, S], F32, name="y_bank%d" % t, tag="y_bank%d" % t)
             pieces = [(bank, 0, n_chunks)]
             if t == 0:
                 late = [ps.tile([P, S], F32, name="y_late%d" % i, tag="h_bank%d" % i) for i in range(2)]

@@ -18,9 +18,9 @@ ACT = mybir.ActivationFunctionType
 P = 128
 PACK = 4
 CHUNK = 128
-W1_VECTOR_M = 52
-W2A_VECTOR_M = 52
-W2B_VECTOR_M = 96
+SCALE_ROWS = 16
+W1_VECTOR_M = 84
+W2_SCALAR_M = 48
 LAST_VECTOR_COLS = 384
 
 
@@ -40,32 +40,28 @@ def tile_picked_ydcons_relu_po_kernel(
             return sb.tile(shape, dtype, name=name, tag=tag or name, align_bytes=64)
 
         x_scale_table = sbuf([P, T], U8, "x_scale_table")
-        nc.vector.memset(x_scale_table[:].bitcast(I32), 0)
+        nc.sync.dma_start(x_scale_table[P - SCALE_ROWS :, :].bitcast(I32), x_scales[0].bitcast(I32))
+        nc.sync.dma_start(offs_sb[:], offs)
+        nc.vector.memset(x_scale_table[: P - SCALE_ROWS, :].bitcast(I32), 0)
+        x_scales_picked = sbuf([P, S], U8, "x_scales_picked")
+        nc.vector.memset(x_scales_picked[:].bitcast(I32), 0)
         quarter = sbuf([P, V], F32, "quarter")
         nc.vector.memset(quarter[:], 0.25)
 
-        nc.sync.dma_start(offs_sb[:], offs)
         w1_raw = sbuf([P, PACK, H], F32, "w1_raw")
         nc.sync.dma_start(w1_raw[:], w1.rearrange("(p j) c -> p j c", j=PACK))
-        for q in range(4):
-            nc.sync.dma_start(
-                x_scale_table[32 * q : 32 * q + 4, :].bitcast(I32),
-                x_scales[0, 4 * q : 4 * q + 4, :].bitcast(I32),
-            )
         x_word_table = sbuf([P, T], U32, "x_word_table")
         nc.sync.dma_start(
             x_word_table[:].bitcast(I32), x_words[0].rearrange("p n t -> p (n t)").bitcast(I32)
         )
-        w2_rows = w2.rearrange("(p j) c -> p j c", j=PACK)
-        w2_raw = []
-        for u in range(2):
-            part = sbuf([P, PACK, N // 2], F32, "w2_raw%d" % u)
-            nc.sync.dma_start(part[:], w2_rows[:, :, u * N // 2 : (u + 1) * N // 2])
-            w2_raw.append(part)
         nc.sync.dma_start(line_sb[:], line)
-        meas_raw = sbuf([P, PACK, V], F32, "meas_raw")
-        nc.sync.dma_start(meas_raw[:], meas.rearrange("(p t) v -> p t v", t=PACK))
-
+        x_scale_rows = sbuf([P, S], U8, "x_scale_rows")
+        nc.vector.tensor_copy(x_scale_rows[:], x_scale_table[:].indirect(offs_sb[:]))
+        for q in range(4):
+            lo = P - SCALE_ROWS + 4 * q
+            nc.sync.dma_start(
+                x_scales_picked[32 * q : 32 * q + 4, :].bitcast(I32), x_scale_rows[lo : lo + 4, :].bitcast(I32)
+            )
         def deal_views(raw, name, t_lo, t_hi, tag=None):
             nt = t_hi - t_lo
             dealt = sbuf([P, nt * P * PACK], BF16, name + "_bf16", tag)
@@ -73,9 +69,9 @@ def tile_picked_ydcons_relu_po_kernel(
             src = raw[:].rearrange("p j (m t) -> p m j t", t=PACK)[:, :, :, t_lo:t_hi]
             return dealt, dst, src
 
-        def quantize(values, name):
+        def quantize(values, name, tag=None):
             width = values.shape[1] // PACK
-            codes = sbuf([P, width], U32, name + "_codes")
+            codes = sbuf([P, width], U32, name + "_codes", tag)
             scales = sbuf([P, width], U8, name + "_scales")
             nc.vector.quantize_mx(out=codes[:].bitcast(FP8X4), scales=scales[:], in_=values)
             return codes, scales
@@ -94,61 +90,73 @@ def tile_picked_ydcons_relu_po_kernel(
         w1_bf16, dst, src = deal_views(w1_raw, "w1", 0, PACK)
         nc.vector.tensor_copy(dst[:, :W1_VECTOR_M], src[:, :W1_VECTOR_M])
         nc.scalar.copy(dst[:, W1_VECTOR_M:], src[:, W1_VECTOR_M:])
-        x_scales_picked = sbuf([P, S], U8, "x_scales_picked")
-        nc.vector.tensor_copy(x_scales_picked[:], x_scale_table[:].indirect(offs_sb[:]))
         w1_q = quantize(w1_bf16[:], "w1")
+        w2_rows = w2.rearrange("(p j) c -> p j c", j=PACK)
+        w2_raw = []
+        for u, (lo, hi) in enumerate(((0, W2_SCALAR_M), (W2_SCALAR_M, P))):
+            part = sbuf([P, PACK, (hi - lo) * PACK], F32, "w2_raw%d" % u, ("x_scale_table", "w1_raw")[u])
+            nc.sync.dma_start(part[:], w2_rows[:, :, lo * PACK : hi * PACK])
+            w2_raw.append(part)
+        meas_raw = sbuf([P, PACK, V], F32, "meas_raw", "x_scale_rows")
+        nc.sync.dma_start(meas_raw[:], meas.rearrange("(p t) v -> p t v", t=PACK))
+
 
         warm = ps.tile([P, S], F32, name="warm", tag="y_bank3")
         for i in range(2):
             product(warm[:], w1_q, slice(i * P, (i + 1) * P), w1_q[0][:], w1_q[1][:])
 
         half = S // 2
-        x_picked = []
+        x_picked = sbuf([P, S], U32, "x_picked", "w1_bf16")
         for u in range(2):
-            words = sbuf([P, half], U32, "x_picked%d" % u)
             nc.vector.tensor_copy(
-                words[:], x_word_table[:].indirect(offs_sb[:, u * half // 16 : (u + 1) * half // 16])
+                x_picked[:, u * half : (u + 1) * half],
+                x_word_table[:].indirect(offs_sb[:, u * half // 16 : (u + 1) * half // 16]),
             )
-            x_picked.append(words)
 
         n_chunks = S // CHUNK
         h_banks = []
         for c in range(n_chunks):
             bank = ps.tile([P, PACK, CHUNK], F32, name="h_bank%d" % c)
-            u, lo = divmod(c * CHUNK, half)
             for t in range(PACK):
                 product(
                     bank[:, t, :],
                     w1_q,
                     slice(t * P, (t + 1) * P),
-                    x_picked[u][:, lo : lo + CHUNK],
+                    x_picked[:, c * CHUNK : (c + 1) * CHUNK],
                     x_scales_picked[:, c * CHUNK : (c + 1) * CHUNK],
                 )
             h_banks.append(bank)
 
-        def relu_out(c):
-            h_bf16 = sbuf([P, CHUNK * PACK], BF16, "h_bf16_%d" % c, "w2_raw1" if c == n_chunks - 1 else None)
-            dst = h_bf16[:].rearrange("p (n t) -> p n t", t=PACK)
+        w2_bf16 = sbuf([P, N * PACK], BF16, "w2_bf16")
+        w2_dealt = w2_bf16[:].rearrange("p (t m j) -> p m j t", t=PACK, j=PACK)
+        nc.scalar.copy(w2_dealt[:, :W2_SCALAR_M], w2_raw[0][:].rearrange("p j (m t) -> p m j t", t=PACK))
+
+        h_first = sbuf([P, CHUNK * PACK], BF16, "h_first")
+        h_rest = sbuf([P, (n_chunks - 1) * CHUNK * PACK], BF16, "h_rest", "x_scale_table")
+        h_bf16 = [h_first[:]] + [h_rest[:, i * CHUNK * PACK : (i + 1) * CHUNK * PACK] for i in range(n_chunks - 1)]
+        for c in range(n_chunks):
+            dst = h_bf16[c].rearrange("p (n t) -> p n t", t=PACK)
             src = h_banks[c][:].rearrange("p t n -> p n t")
-            if c < n_chunks - 1:
+            if c == 0:
                 nc.vector.tensor_scalar_max(dst, src, 0.0)
             else:
                 nc.scalar.activation(dst, src, ACT.Relu)
-            return h_bf16
 
-        w2_bf16 = sbuf([P, N * PACK], BF16, "w2_bf16")
-        w2_dealt = w2_bf16[:].rearrange("p (t m j) -> p m j t", t=PACK, j=PACK)
-        for u in range(2):
-            nc.scalar.copy(
-                w2_dealt[:, u * P // 2 : (u + 1) * P // 2],
-                w2_raw[u][:].rearrange("p j (m t) -> p m j t", t=PACK),
-            )
-        h_bf16 = [relu_out(c) for c in range(n_chunks)]
-        h_q = [quantize(h_bf16[c][:], "h%d" % c) for c in range(n_chunks - 1)]
+        h_codes = sbuf([P, S], U32, "h_codes")
+        h_scales = sbuf([P, S], U8, "h_scales")
+
+        def quantize_h(c):
+            cols = slice(c * CHUNK, (c + 1) * CHUNK)
+            nc.vector.quantize_mx(out=h_codes[:, cols].bitcast(FP8X4), scales=h_scales[:, cols], in_=h_bf16[c])
+
+        quantize_h(0)
+        nc.vector.tensor_copy(w2_dealt[:, W2_SCALAR_M:], w2_raw[1][:].rearrange("p j (m t) -> p m j t", t=PACK))
+        quantize_h(1)
         w2_q0 = quantize(w2_bf16[:, : P * PACK], "w2t0")
-        h_q.append(quantize(h_bf16[n_chunks - 1][:], "h3"))
-        w2_q1 = quantize(w2_bf16[:, P * PACK : 2 * P * PACK], "w2t1")
-        w2_qb = quantize(w2_bf16[:, 2 * P * PACK :], "w2b")
+        quantize_h(2)
+        quantize_h(3)
+        w2_q1 = quantize(w2_bf16[:, P * PACK : 2 * P * PACK], "w2t1", "x_scale_table")
+        w2_qb = quantize(w2_bf16[:, 2 * P * PACK :], "w2b", "h_first")
 
         out_bf16 = sbuf([P, S, PACK], BF16, "out_bf16")
         out_rows = out_0.rearrange("(p t) n -> p t n", t=PACK)
@@ -162,25 +170,24 @@ def tile_picked_ydcons_relu_po_kernel(
                 late = [ps.tile([P, S], F32, name="y_late%d" % i, tag="h_bank%d" % i) for i in range(2)]
                 pieces = [(bank, 0, 2), (late[0], 2, 3), (late[1], 3, 4)]
             for piece, lo, hi in pieces:
-                for c in range(lo, hi):
-                    product(piece[:, c * CHUNK : (c + 1) * CHUNK], weights, w_cols, h_q[c][0][:], h_q[c][1][:])
-                nc.scalar.copy(y[:, lo * CHUNK : hi * CHUNK], piece[:, lo * CHUNK : hi * CHUNK])
+                cols = slice(lo * CHUNK, hi * CHUNK)
+                product(piece[:, cols], weights, w_cols, h_codes[:, cols], h_scales[:, cols])
+                nc.scalar.copy(y[:, cols], piece[:, cols])
             y_tiles.append(y)
 
-        meas_part = [None] * PACK
+        meas_part = []
 
-        def weigh_meas(t, tag=None):
-            meas_part[t] = sbuf([P, V], F32, "meas_part%d" % t, tag)
-            nc.scalar.mul(meas_part[t][:], meas_raw[:, t, :], 0.75)
+        def weigh_meas(pair, tag):
+            part = sbuf([P, 2, V], F32, "meas_part%d" % pair, tag)
+            nc.scalar.mul(part[:], meas_raw[:, 2 * pair : 2 * pair + 2, :], 0.75)
+            meas_part.extend([part[:, 0, :], part[:, 1, :]])
 
         second_layer(0, w2_q0, slice(0, P))
         second_layer(1, w2_q1, slice(0, P))
-        weigh_meas(0, "w2t1_codes")
-        weigh_meas(1, "w2t0_codes")
+        weigh_meas(0, "x_scale_table")
         second_layer(2, w2_qb, slice(0, P))
         second_layer(3, w2_qb, slice(P, 2 * P))
-        weigh_meas(2, "w2b_codes")
-        weigh_meas(3, "w2b_scales")
+        weigh_meas(1, "h_first")
 
         picked = [sbuf([P, V], F32, "picked%d" % t) for t in range(PACK)]
         for pair in range(0, PACK, 2):
@@ -188,7 +195,7 @@ def tile_picked_ydcons_relu_po_kernel(
                 nc.vector.tensor_tensor(picked[t][:], y_tiles[t][:].indirect(line_sb[:]), quarter[:], ALU.mult)
             for t in (pair, pair + 1):
                 y = y_tiles[t]
-                nc.vector.tensor_tensor(y[:].indirect(line_sb[:]), picked[t][:], meas_part[t][:], ALU.add)
+                nc.vector.tensor_tensor(y[:].indirect(line_sb[:]), picked[t][:], meas_part[t], ALU.add)
                 nc.sync.dma_start(out_rows[:, t, :], y[:])
                 if t < PACK - 2:
                     nc.scalar.copy(out_bf16[:, :, t], y[:])

@@ -18,6 +18,7 @@ ACT = mybir.ActivationFunctionType
 P = 128
 PACK = 4
 CHUNK = 128
+ORDER = (1, 2, 0, 3)
 SCALE_ROWS = 16
 W1_VECTOR_M = 84
 W2_SCALAR_M = 48
@@ -150,57 +151,65 @@ def tile_picked_ydcons_relu_po_kernel(
             nc.vector.quantize_mx(out=h_codes[:, cols].bitcast(FP8X4), scales=h_scales[:, cols], in_=h_bf16[c])
 
         quantize_h(0)
-        nc.vector.tensor_copy(w2_dealt[:, W2_SCALAR_M:], w2_raw[1][:].rearrange("p j (m t) -> p m j t", t=PACK))
+        w2_late = w2_raw[1][:].rearrange("p j (m t) -> p m j t", t=PACK)
+        nc.vector.tensor_copy(w2_dealt[:, W2_SCALAR_M:, :, 1:3], w2_late[:, :, :, 1:3])
         quantize_h(1)
-        w2_q0 = quantize(w2_bf16[:, : P * PACK], "w2t0")
+        w2_qa = quantize(w2_bf16[:, P * PACK : 3 * P * PACK], "w2a")
         quantize_h(2)
         quantize_h(3)
-        w2_q1 = quantize(w2_bf16[:, P * PACK : 2 * P * PACK], "w2t1", "x_scale_table")
-        w2_qb = quantize(w2_bf16[:, 2 * P * PACK :], "w2b", "h_first")
+        nc.vector.tensor_copy(w2_dealt[:, W2_SCALAR_M:, :, ::3], w2_late[:, :, :, ::3])
+        w2_q0 = quantize(w2_bf16[:, : P * PACK], "w2t0")
+        w2_q3 = quantize(w2_bf16[:, 3 * P * PACK :], "w2t3")
 
         out_bf16 = sbuf([P, S, PACK], BF16, "out_bf16")
         out_rows = out_0.rearrange("(p t) n -> p t n", t=PACK)
-        y_tiles = []
+        y_tiles = {}
 
         def second_layer(t, weights, w_cols):
             y = sbuf([P, S], F32, "y%d" % t)
             bank = ps.tile([P, S], F32, name="y_bank%d" % t, tag="y_bank%d" % t)
             pieces = [(bank, 0, n_chunks)]
-            if t == 0:
+            if t == ORDER[0]:
                 late = [ps.tile([P, S], F32, name="y_late%d" % i, tag="h_bank%d" % i) for i in range(2)]
                 pieces = [(bank, 0, 2), (late[0], 2, 3), (late[1], 3, 4)]
+            if t == ORDER[1]:
+                pieces = [(bank, 0, 2), (ps.tile([P, S], F32, name="y1_late", tag="h_bank2"), 2, 4)]
             for piece, lo, hi in pieces:
                 cols = slice(lo * CHUNK, hi * CHUNK)
                 product(piece[:, cols], weights, w_cols, h_codes[:, cols], h_scales[:, cols])
                 nc.scalar.copy(y[:, cols], piece[:, cols])
-            y_tiles.append(y)
+            y_tiles[t] = y
 
-        meas_part = []
+        meas_part = {}
 
-        def weigh_meas(pair, tag):
-            part = sbuf([P, 2, V], F32, "meas_part%d" % pair, tag)
-            nc.scalar.mul(part[:], meas_raw[:, 2 * pair : 2 * pair + 2, :], 0.75)
-            meas_part.extend([part[:, 0, :], part[:, 1, :]])
+        def weigh_meas(rows, name, tag):
+            part = sbuf([P, 2, V], F32, name, tag)
+            nc.scalar.mul(part[:], meas_raw[:, rows, :], 0.75)
+            for i, t in enumerate(range(PACK)[rows]):
+                meas_part[t] = part[:, i, :]
 
+        second_layer(1, w2_qa, slice(0, P))
+        second_layer(2, w2_qa, slice(P, 2 * P))
+        weigh_meas(slice(1, 3), "meas_inner", "w2a_codes")
         second_layer(0, w2_q0, slice(0, P))
-        second_layer(1, w2_q1, slice(0, P))
-        weigh_meas(0, "x_scale_table")
-        second_layer(2, w2_qb, slice(0, P))
-        second_layer(3, w2_qb, slice(P, 2 * P))
-        weigh_meas(1, "h_first")
+        second_layer(3, w2_q3, slice(0, P))
+        weigh_meas(slice(0, PACK, 3), "meas_outer", "w2t3_codes")
 
         picked = [sbuf([P, V], F32, "picked%d" % t) for t in range(PACK)]
-        for pair in range(0, PACK, 2):
-            for t in (pair, pair + 1):
+        for pair in (ORDER[:2], ORDER[2:]):
+            for t in pair:
                 nc.vector.tensor_tensor(picked[t][:], y_tiles[t][:].indirect(line_sb[:]), quarter[:], ALU.mult)
-            for t in (pair, pair + 1):
+            for t in pair:
                 y = y_tiles[t]
                 nc.vector.tensor_tensor(y[:].indirect(line_sb[:]), picked[t][:], meas_part[t], ALU.add)
                 nc.sync.dma_start(out_rows[:, t, :], y[:])
-                if t < PACK - 2:
+                if t == 1:
                     nc.scalar.copy(out_bf16[:, :, t], y[:])
-                elif t == PACK - 2:
+                elif t == 2:
                     nc.scalar.copy(out_bf16[:, :, t:], y[:].unsqueeze(2).to_broadcast([P, S, 2]))
+                elif t == 0:
+                    nc.scalar.copy(out_bf16[:, :half, t], y[:, :half])
+                    nc.scalar.copy(out_bf16[:, half:, t], y[:, half:])
                 else:
                     nc.vector.tensor_copy(out_bf16[:, :half, t], y[:, :half])
                     nc.vector.tensor_copy(out_bf16[:, half:LAST_VECTOR_COLS, t], y[:, half:LAST_VECTOR_COLS])

@@ -47,7 +47,9 @@ def tile_picked_ydcons_relu_po_kernel(
         x_scales_picked = sbuf([P, S], U8, "x_scales_picked")
         nc.vector.memset(x_scales_picked[:].bitcast(I32), 0)
         quarter = sbuf([P, V], F32, "quarter")
-        nc.vector.memset(quarter[:], 0.25)
+        ones = sbuf([P, V], F32, "ones")
+        nc.vector.memset(ones[:], 1.0)
+        nc.scalar.mul(quarter[:], ones[:], 0.25)
 
         w1_raw = sbuf([P, PACK, H], F32, "w1_raw")
         nc.sync.dma_start(w1_raw[:], w1.rearrange("(p j) c -> p j c", j=PACK))
@@ -60,7 +62,7 @@ def tile_picked_ydcons_relu_po_kernel(
         nc.vector.tensor_copy(x_scale_rows[:], x_scale_table[:].indirect(offs_sb[:]))
         for q in range(4):
             lo = P - SCALE_ROWS + 4 * q
-            nc.sync.dma_start(
+            nc.scalar.dma_start(
                 x_scales_picked[32 * q : 32 * q + 4, :].bitcast(I32), x_scale_rows[lo : lo + 4, :].bitcast(I32)
             )
         def deal_views(raw, name, t_lo, t_hi, tag=None):

@@ -41,7 +41,7 @@ def tile_picked_ydcons_relu_po_kernel(
             return sb.tile(shape, dtype, name=name, tag=tag or name, align_bytes=64)
 
         x_scale_table = sbuf([P, T], U8, "x_scale_table")
-        nc.sync.dma_start(x_scale_table[P - SCALE_ROWS :, :].bitcast(I32), x_scales[0].bitcast(I32))
+        nc.scalar.dma_start(x_scale_table[P - SCALE_ROWS :, :].bitcast(I32), x_scales[0].bitcast(I32))
         nc.sync.dma_start(offs_sb[:], offs)
         nc.vector.memset(x_scale_table[: P - SCALE_ROWS, :].bitcast(I32), 0)
         x_scales_picked = sbuf([P, S], U8, "x_scales_picked")

@@ -104,10 +104,6 @@ def tile_picked_ydcons_relu_po_kernel(
         nc.sync.dma_start(meas_raw[:], meas.rearrange("(p t) v -> p t v", t=PACK))
 
 
-        warm = ps.tile([P, S], F32, name="warm", tag="y_bank3")
-        for i in range(2):
-            product(warm[:], w1_q, slice(i * P, (i + 1) * P), w1_q[0][:], w1_q[1][:])
-
         half = S // 2
         x_picked = sbuf([P, S], U32, "x_picked", "w1_bf16")
         for u in range(2):

@@ -18,10 +18,8 @@ ACT = mybir.ActivationFunctionType
 P = 128
 PACK = 4
 CHUNK = 128
-ORDER = (1, 2, 0, 3)
 SCALE_ROWS = 16
 W1_VECTOR_M = 84
-W2_SCALAR_M = 48
 LAST_VECTOR_COLS = 384
 
 
@@ -47,9 +45,9 @@ def tile_picked_ydcons_relu_po_kernel(
         x_scales_picked = sbuf([P, S], U8, "x_scales_picked")
         nc.vector.memset(x_scales_picked[:].bitcast(I32), 0)
         quarter = sbuf([P, V], F32, "quarter")
-        ones = sbuf([P, V], F32, "ones")
+        ones = sbuf([P, V // 2], F32, "ones")
         nc.vector.memset(ones[:], 1.0)
-        nc.scalar.mul(quarter[:], ones[:], 0.25)
+        nc.scalar.mul(quarter[:, : V // 2], ones[:], 0.25)
 
         w1_raw = sbuf([P, PACK, H], F32, "w1_raw")
         nc.sync.dma_start(w1_raw[:], w1.rearrange("(p j) c -> p j c", j=PACK))
@@ -65,6 +63,10 @@ def tile_picked_ydcons_relu_po_kernel(
             nc.scalar.dma_start(
                 x_scales_picked[32 * q : 32 * q + 4, :].bitcast(I32), x_scale_rows[lo : lo + 4, :].bitcast(I32)
             )
+        late_ones = sbuf([P, V // 2], F32, "late_ones", "x_scale_table")
+        nc.vector.memset(late_ones[:], 1.0)
+        nc.scalar.mul(quarter[:, V // 2 :], late_ones[:], 0.25)
+
         def deal_views(raw, name, t_lo, t_hi, tag=None):
             nt = t_hi - t_lo
             dealt = sbuf([P, nt * P * PACK], BF16, name + "_bf16", tag)
@@ -94,12 +96,8 @@ def tile_picked_ydcons_relu_po_kernel(
         nc.vector.tensor_copy(dst[:, :W1_VECTOR_M], src[:, :W1_VECTOR_M])
         nc.scalar.copy(dst[:, W1_VECTOR_M:], src[:, W1_VECTOR_M:])
         w1_q = quantize(w1_bf16[:], "w1")
-        w2_rows = w2.rearrange("(p j) c -> p j c", j=PACK)
-        w2_raw = []
-        for u, (lo, hi) in enumerate(((0, W2_SCALAR_M), (W2_SCALAR_M, P))):
-            part = sbuf([P, PACK, (hi - lo) * PACK], F32, "w2_raw%d" % u, ("x_scale_table", "w1_raw")[u])
-            nc.sync.dma_start(part[:], w2_rows[:, :, lo * PACK : hi * PACK])
-            w2_raw.append(part)
+        w2_raw = sbuf([P, PACK, N], F32, "w2_raw", "x_scale_table")
+        nc.sync.dma_start(w2_raw[:], w2.rearrange("(p j) c -> p j c", j=PACK))
         meas_raw = sbuf([P, PACK, V], F32, "meas_raw", "x_scale_rows")
         nc.sync.dma_start(meas_raw[:], meas.rearrange("(p t) v -> p t v", t=PACK))
 
@@ -126,51 +124,40 @@ def tile_picked_ydcons_relu_po_kernel(
                 )
             h_banks.append(bank)
 
-        w2_bf16 = sbuf([P, N * PACK], BF16, "w2_bf16")
-        w2_dealt = w2_bf16[:].rearrange("p (t m j) -> p m j t", t=PACK, j=PACK)
-        nc.scalar.copy(w2_dealt[:, :W2_SCALAR_M], w2_raw[0][:].rearrange("p j (m t) -> p m j t", t=PACK))
-
-        h_first = sbuf([P, CHUNK * PACK], BF16, "h_first")
-        h_rest = sbuf([P, (n_chunks - 1) * CHUNK * PACK], BF16, "h_rest", "x_scale_table")
-        h_bf16 = [h_first[:]] + [h_rest[:, i * CHUNK * PACK : (i + 1) * CHUNK * PACK] for i in range(n_chunks - 1)]
+        h_bf16 = [sbuf([P, CHUNK * PACK], BF16, "h_bf16_%d" % c) for c in range(n_chunks)]
         for c in range(n_chunks):
-            dst = h_bf16[c].rearrange("p (n t) -> p n t", t=PACK)
+            dst = h_bf16[c][:].rearrange("p (n t) -> p n t", t=PACK)
             src = h_banks[c][:].rearrange("p t n -> p n t")
-            if c == 0:
-                nc.vector.tensor_scalar_max(dst, src, 0.0)
-            else:
-                nc.scalar.activation(dst, src, ACT.Relu)
+            nc.scalar.activation(dst, src, ACT.Relu)
 
-        h_codes = sbuf([P, S], U32, "h_codes")
+        w2_low, dst_low, src_low = deal_views(w2_raw, "w2_low", 0, 2)
+        w2_high, dst_high, src_high = deal_views(w2_raw, "w2_high", 2, PACK)
         h_scales = sbuf([P, S], U8, "h_scales")
 
-        def quantize_h(c):
+        nc.vector.tensor_copy(dst_low, src_low)
+        w2_q_low = quantize(w2_low[:], "w2_low")
+        h_codes = sbuf([P, S], U32, "h_codes", "w2_low_bf16")
+        for c in range(n_chunks):
             cols = slice(c * CHUNK, (c + 1) * CHUNK)
-            nc.vector.quantize_mx(out=h_codes[:, cols].bitcast(FP8X4), scales=h_scales[:, cols], in_=h_bf16[c])
-
-        quantize_h(0)
-        w2_late = w2_raw[1][:].rearrange("p j (m t) -> p m j t", t=PACK)
-        nc.vector.tensor_copy(w2_dealt[:, W2_SCALAR_M:, :, 1:3], w2_late[:, :, :, 1:3])
-        quantize_h(1)
-        w2_qa = quantize(w2_bf16[:, P * PACK : 3 * P * PACK], "w2a")
-        quantize_h(2)
-        quantize_h(3)
-        nc.vector.tensor_copy(w2_dealt[:, W2_SCALAR_M:, :, ::3], w2_late[:, :, :, ::3])
-        w2_q0 = quantize(w2_bf16[:, : P * PACK], "w2t0")
-        w2_q3 = quantize(w2_bf16[:, 3 * P * PACK :], "w2t3")
+            nc.vector.quantize_mx(out=h_codes[:, cols].bitcast(FP8X4), scales=h_scales[:, cols], in_=h_bf16[c][:])
+        nc.vector.tensor_copy(dst_high[:, : P // 2], src_high[:, : P // 2])
+        nc.vector.tensor_copy(dst_high[:, P // 2 :], src_high[:, P // 2 :])
+        w2_q_high = quantize(w2_high[:], "w2_high")
 
         out_bf16 = sbuf([P, S, PACK], BF16, "out_bf16")
         out_rows = out_0.rearrange("(p t) n -> p t n", t=PACK)
         y_tiles = {}
 
-        def second_layer(t, weights, w_cols):
+        def second_layer(t):
+            weights = (w2_q_low, w2_q_high)[t // 2]
+            w_cols = slice(t % 2 * P, (t % 2 + 1) * P)
             y = sbuf([P, S], F32, "y%d" % t)
             bank = ps.tile([P, S], F32, name="y_bank%d" % t, tag="y_bank%d" % t)
             pieces = [(bank, 0, n_chunks)]
-            if t == ORDER[0]:
+            if t == 0:
                 late = [ps.tile([P, S], F32, name="y_late%d" % i, tag="h_bank%d" % i) for i in range(2)]
                 pieces = [(bank, 0, 2), (late[0], 2, 3), (late[1], 3, 4)]
-            if t == ORDER[1]:
+            if t == 1:
                 pieces = [(bank, 0, 2), (ps.tile([P, S], F32, name="y1_late", tag="h_bank2"), 2, 4)]
             for piece, lo, hi in pieces:
                 cols = slice(lo * CHUNK, hi * CHUNK)
@@ -181,37 +168,49 @@ def tile_picked_ydcons_relu_po_kernel(
         meas_part = {}
 
         def weigh_meas(rows, name, tag):
-            part = sbuf([P, 2, V], F32, name, tag)
+            tiles = range(PACK)[rows]
+            part = sbuf([P, len(tiles), V], F32, name, tag)
             nc.scalar.mul(part[:], meas_raw[:, rows, :], 0.75)
-            for i, t in enumerate(range(PACK)[rows]):
+            for i, t in enumerate(tiles):
                 meas_part[t] = part[:, i, :]
 
-        second_layer(1, w2_qa, slice(0, P))
-        second_layer(2, w2_qa, slice(P, 2 * P))
-        weigh_meas(slice(1, 3), "meas_inner", "w2a_codes")
-        second_layer(0, w2_q0, slice(0, P))
-        second_layer(3, w2_q3, slice(0, P))
-        weigh_meas(slice(0, PACK, 3), "meas_outer", "w2t3_codes")
+        second_layer(0)
+        second_layer(1)
+        weigh_meas(slice(0, 1), "meas_0", "w2_low_codes")
+        second_layer(2)
+        second_layer(3)
+        weigh_meas(slice(2, 3), "meas_2", "w2_high_codes")
+        weigh_meas(slice(1, PACK, 2), "meas_odd", "w2_low_bf16")
 
         picked = [sbuf([P, V], F32, "picked%d" % t) for t in range(PACK)]
-        for pair in (ORDER[:2], ORDER[2:]):
-            for t in pair:
-                nc.vector.tensor_tensor(picked[t][:], y_tiles[t][:].indirect(line_sb[:]), quarter[:], ALU.mult)
-            for t in pair:
-                y = y_tiles[t]
-                nc.vector.tensor_tensor(y[:].indirect(line_sb[:]), picked[t][:], meas_part[t], ALU.add)
-                nc.sync.dma_start(out_rows[:, t, :], y[:])
-                if t == 1:
-                    nc.scalar.copy(out_bf16[:, :, t], y[:])
-                elif t == 2:
-                    nc.scalar.copy(out_bf16[:, :, t:], y[:].unsqueeze(2).to_broadcast([P, S, 2]))
-                elif t == 0:
-                    nc.scalar.copy(out_bf16[:, :half, t], y[:, :half])
-                    nc.scalar.copy(out_bf16[:, half:, t], y[:, half:])
-                else:
-                    nc.vector.tensor_copy(out_bf16[:, :half, t], y[:, :half])
-                    nc.vector.tensor_copy(out_bf16[:, half:LAST_VECTOR_COLS, t], y[:, half:LAST_VECTOR_COLS])
-                    nc.scalar.copy(out_bf16[:, LAST_VECTOR_COLS:, t], y[:, LAST_VECTOR_COLS:])
+
+        def fetch(t):
+            nc.vector.tensor_tensor(picked[t][:], y_tiles[t][:].indirect(line_sb[:]), quarter[:], ALU.mult)
+
+        def put_back(t):
+            y = y_tiles[t]
+            nc.vector.tensor_tensor(y[:].indirect(line_sb[:]), picked[t][:], meas_part[t], ALU.add)
+            nc.sync.dma_start(out_rows[:, t, :], y[:])
+            if t == 0:
+                nc.scalar.copy(out_bf16[:, :, t], y[:])
+            elif t == 2:
+                nc.scalar.copy(out_bf16[:, :, t:], y[:].unsqueeze(2).to_broadcast([P, S, 2]))
+            elif t == 1:
+                nc.scalar.copy(out_bf16[:, :half, t], y[:, :half])
+                nc.scalar.copy(out_bf16[:, half:, t], y[:, half:])
+            else:
+                nc.vector.tensor_copy(out_bf16[:, :half, t], y[:, :half])
+                nc.vector.tensor_copy(out_bf16[:, half:LAST_VECTOR_COLS, t], y[:, half:LAST_VECTOR_COLS])
+                nc.scalar.copy(out_bf16[:, LAST_VECTOR_COLS:, t], y[:, LAST_VECTOR_COLS:])
+
+        fetch(0)
+        fetch(1)
+        put_back(0)
+        fetch(2)
+        fetch(3)
+        put_back(2)
+        put_back(1)
+        put_back(3)
 
         out_codes = sbuf([P, S], U32, "out_codes")
         out_scales = sbuf([P, S], U8, "out_scales")

@@ -224,7 +224,7 @@ def tile_picked_ydcons_relu_po_kernel(
             )
             nc.sync.dma_start(out_words[:, cols], out_codes[:, cols].bitcast(I32))
         for q in range(4):
-            queue = nc.scalar if q % 2 == 0 else nc.sync
+            queue = nc.scalar if q == 0 else nc.sync
             queue.dma_start(
                 out_2[0, 4 * q : 4 * q + 4, :].bitcast(I32),
                 out_scales[32 * q : 32 * q + 4, :].bitcast(I32),

@@ -20,7 +20,6 @@ PACK = 4
 CHUNK = 128
 SCALE_ROWS = 16
 W1_VECTOR_M = 84
-LAST_VECTOR_COLS = 384
 
 
 def tile_picked_ydcons_relu_po_kernel(
@@ -144,11 +143,12 @@ def tile_picked_ydcons_relu_po_kernel(
         nc.vector.tensor_copy(dst_high[:, P // 2 :], src_high[:, P // 2 :])
         w2_q_high = quantize(w2_high[:], "w2_high")
 
-        out_bf16 = sbuf([P, S, PACK], BF16, "out_bf16")
         out_rows = out_0.rearrange("(p t) n -> p t n", t=PACK)
+        meas3 = sbuf([P, PACK, V], F32, "meas3")
+        nc.vector.tensor_scalar(meas3[:], meas_raw[:], 3.0, None, ALU.mult)
         y_tiles = {}
 
-        def second_layer(t):
+        def second_layer(t, engine_copy):
             weights = (w2_q_low, w2_q_high)[t // 2]
             w_cols = slice(t % 2 * P, (t % 2 + 1) * P)
             y = sbuf([P, S], F32, "y%d" % t)
@@ -162,66 +162,56 @@ def tile_picked_ydcons_relu_po_kernel(
             for piece, lo, hi in pieces:
                 cols = slice(lo * CHUNK, hi * CHUNK)
                 product(piece[:, cols], weights, w_cols, h_codes[:, cols], h_scales[:, cols])
-                nc.scalar.copy(y[:, cols], piece[:, cols])
+                engine_copy(y[:, cols], piece[:, cols])
             y_tiles[t] = y
 
-        meas_part = {}
-
-        def weigh_meas(rows, name, tag):
-            tiles = range(PACK)[rows]
-            part = sbuf([P, len(tiles), V], F32, name, tag)
-            nc.scalar.mul(part[:], meas_raw[:, rows, :], 0.75)
-            for i, t in enumerate(tiles):
-                meas_part[t] = part[:, i, :]
-
-        second_layer(0)
-        second_layer(1)
-        weigh_meas(slice(0, 1), "meas_0", "w2_low_codes")
-        second_layer(2)
-        second_layer(3)
-        weigh_meas(slice(2, 3), "meas_2", "w2_high_codes")
-        weigh_meas(slice(1, PACK, 2), "meas_odd", "w2_low_bf16")
-
         picked = [sbuf([P, V], F32, "picked%d" % t) for t in range(PACK)]
+        pairs = sbuf([P, 2, S, 2], BF16, "pairs")
 
         def fetch(t):
-            nc.vector.tensor_tensor(picked[t][:], y_tiles[t][:].indirect(line_sb[:]), quarter[:], ALU.mult)
+            nc.vector.tensor_tensor(picked[t][:], y_tiles[t][:].indirect(line_sb[:]), meas3[:, t, :], ALU.add)
 
-        def put_back(t):
+        def put_back(t, on_vector):
             y = y_tiles[t]
-            nc.vector.tensor_tensor(y[:].indirect(line_sb[:]), picked[t][:], meas_part[t], ALU.add)
-            nc.sync.dma_start(out_rows[:, t, :], y[:])
-            if t == 0:
-                nc.scalar.copy(out_bf16[:, :, t], y[:])
-            elif t == 2:
-                nc.scalar.copy(out_bf16[:, :, t:], y[:].unsqueeze(2).to_broadcast([P, S, 2]))
-            elif t == 1:
-                nc.scalar.copy(out_bf16[:, :half, t], y[:, :half])
-                nc.scalar.copy(out_bf16[:, half:, t], y[:, half:])
+            if on_vector:
+                nc.vector.tensor_tensor(y[:].indirect(line_sb[:]), picked[t][:], quarter[:], ALU.mult)
             else:
-                nc.vector.tensor_copy(out_bf16[:, :half, t], y[:, :half])
-                nc.vector.tensor_copy(out_bf16[:, half:LAST_VECTOR_COLS, t], y[:, half:LAST_VECTOR_COLS])
-                nc.scalar.copy(out_bf16[:, LAST_VECTOR_COLS:, t], y[:, LAST_VECTOR_COLS:])
+                nc.scalar.activation(y[:].indirect(line_sb[:]), picked[t][:], ACT.Copy, scale=0.25)
+            nc.sync.dma_start(out_rows[:, t, :], y[:])
 
+        def round_rows(t, cols):
+            nc.vector.tensor_copy(pairs[:, t // 2, cols, t % 2], y_tiles[t][:, cols])
+
+        second_layer(0, nc.scalar.copy)
+        second_layer(1, nc.scalar.copy)
+        second_layer(2, nc.scalar.copy)
         fetch(0)
+        second_layer(3, nc.vector.tensor_copy)
         fetch(1)
-        put_back(0)
         fetch(2)
         fetch(3)
-        put_back(2)
-        put_back(1)
-        put_back(3)
+        put_back(0, False)
+        put_back(1, False)
+        put_back(2, True)
+        put_back(3, False)
+        halves = [slice(u * half, (u + 1) * half) for u in range(2)]
+        for t in range(PACK - 1):
+            round_rows(t, slice(0, S))
+        for cols in halves:
+            round_rows(PACK - 1, cols)
 
         out_codes = sbuf([P, S], U32, "out_codes")
         out_scales = sbuf([P, S], U8, "out_scales")
         out_words = out_1[0].rearrange("p n t -> p (n t)").bitcast(I32)
-        for u in range(2):
-            cols = slice(u * half, (u + 1) * half)
-            nc.vector.quantize_mx(
-                out=out_codes[:, cols].bitcast(FP8X4),
-                scales=out_scales[:, cols],
-                in_=out_bf16[:, cols, :].rearrange("p n t -> p (n t)"),
+        pair_words = pairs[:].rearrange("p a n b -> p a (n b)").bitcast(I32)
+        out_bf16 = [sbuf([P, half * PACK], BF16, "out_bf16_%d" % u) for u in range(2)]
+        for u, cols in enumerate(halves):
+            nc.vector.tensor_copy(
+                out_bf16[u][:].bitcast(I32).rearrange("p (n a) -> p n a", a=2),
+                pair_words[:, :, cols].rearrange("p a n -> p n a"),
             )
+        for u, cols in enumerate(halves):
+            nc.vector.quantize_mx(out=out_codes[:, cols].bitcast(FP8X4), scales=out_scales[:, cols], in_=out_bf16[u][:])
             nc.sync.dma_start(out_words[:, cols], out_codes[:, cols].bitcast(I32))
         for q in range(4):
             queue = nc.scalar if q == 0 else nc.sync

@@ -20,6 +20,7 @@ PACK = 4
 CHUNK = 128
 SCALE_ROWS = 16
 W1_VECTOR_M = 84
+VECTOR_COLS = 384
 
 
 def tile_picked_ydcons_relu_po_kernel(
@@ -166,7 +167,6 @@ def tile_picked_ydcons_relu_po_kernel(
             y_tiles[t] = y
 
         picked = [sbuf([P, V], F32, "picked%d" % t) for t in range(PACK)]
-        pairs = sbuf([P, 2, S, 2], BF16, "pairs")
 
         def fetch(t):
             nc.vector.tensor_tensor(picked[t][:], y_tiles[t][:].indirect(line_sb[:]), meas3[:, t, :], ALU.add)
@@ -179,8 +179,9 @@ def tile_picked_ydcons_relu_po_kernel(
                 nc.scalar.activation(y[:].indirect(line_sb[:]), picked[t][:], ACT.Copy, scale=0.25)
             nc.sync.dma_start(out_rows[:, t, :], y[:])
 
-        def round_rows(t, cols):
-            nc.vector.tensor_copy(pairs[:, t // 2, cols, t % 2], y_tiles[t][:, cols])
+        def round_rows(t, lo, hi, engine_copy):
+            rows = pairs[:].rearrange("p (a n b) -> p a n b", a=2, b=2)
+            engine_copy(rows[:, t // 2, lo:hi, t % 2], y_tiles[t][:, lo:hi])
 
         second_layer(0, nc.scalar.copy)
         second_layer(1, nc.scalar.copy)
@@ -188,28 +189,37 @@ def tile_picked_ydcons_relu_po_kernel(
         fetch(0)
         second_layer(3, nc.vector.tensor_copy)
         fetch(1)
-        fetch(2)
         fetch(3)
+        fetch(2)
         put_back(0, False)
         put_back(1, False)
-        put_back(2, True)
-        put_back(3, False)
+        put_back(2, False)
+        put_back(3, True)
         halves = [slice(u * half, (u + 1) * half) for u in range(2)]
-        for t in range(PACK - 1):
-            round_rows(t, slice(0, S))
-        for cols in halves:
-            round_rows(PACK - 1, cols)
-
         out_codes = sbuf([P, S], U32, "out_codes")
         out_scales = sbuf([P, S], U8, "out_scales")
         out_words = out_1[0].rearrange("p n t -> p (n t)").bitcast(I32)
-        pair_words = pairs[:].rearrange("p a n b -> p a (n b)").bitcast(I32)
+        pairs = sbuf([P, 2 * S * 2], BF16, "pairs", "meas3")
+        round_rows(0, 0, S, nc.vector.tensor_copy)
+        round_rows(1, 0, S, nc.vector.tensor_copy)
+        round_rows(3, 0, VECTOR_COLS, nc.vector.tensor_copy)
+        round_rows(2, 0, half, nc.vector.tensor_copy)
+        round_rows(2, half, VECTOR_COLS, nc.vector.tensor_copy)
+        round_rows(3, VECTOR_COLS, S, nc.scalar.copy)
+        round_rows(2, VECTOR_COLS, S, nc.scalar.copy)
         out_bf16 = [sbuf([P, half * PACK], BF16, "out_bf16_%d" % u) for u in range(2)]
-        for u, cols in enumerate(halves):
-            nc.vector.tensor_copy(
-                out_bf16[u][:].bitcast(I32).rearrange("p (n a) -> p n a", a=2),
-                pair_words[:, :, cols].rearrange("p a n -> p n a"),
+
+        def weave(lo, hi, engine_copy, dtype):
+            u = lo // half
+            words = out_bf16[u][:].bitcast(dtype)[:, 2 * (lo - u * half) : 2 * (hi - u * half)]
+            engine_copy(
+                words.rearrange("p (n a) -> p n a", a=2),
+                pairs[:].bitcast(dtype).rearrange("p (a n) -> p n a", a=2)[:, lo:hi],
             )
+
+        weave(0, half, nc.vector.tensor_copy, I32)
+        weave(half, VECTOR_COLS, nc.vector.tensor_copy, I32)
+        weave(VECTOR_COLS, S, nc.scalar.copy, U32)
         for u, cols in enumerate(halves):
             nc.vector.quantize_mx(out=out_codes[:, cols].bitcast(FP8X4), scales=out_scales[:, cols], in_=out_bf16[u][:])
             nc.sync.dma_start(out_words[:, cols], out_codes[:, cols].bitcast(I32))

@@ -104,11 +104,8 @@ def tile_picked_ydcons_relu_po_kernel(
 
         half = S // 2
         x_picked = sbuf([P, S], U32, "x_picked", "w1_bf16")
-        for u in range(2):
-            nc.vector.tensor_copy(
-                x_picked[:, u * half : (u + 1) * half],
-                x_word_table[:].indirect(offs_sb[:, u * half // 16 : (u + 1) * half // 16]),
-            )
+        for lo, hi in ((0, CHUNK), (CHUNK, half), (half, S)):
+            nc.vector.tensor_copy(x_picked[:, lo:hi], x_word_table[:].indirect(offs_sb[:, lo // 16 : hi // 16]))
 
         n_chunks = S // CHUNK
         h_banks = []

@@ -45,9 +45,9 @@ def tile_picked_ydcons_relu_po_kernel(
         x_scales_picked = sbuf([P, S], U8, "x_scales_picked")
         nc.vector.memset(x_scales_picked[:].bitcast(I32), 0)
         quarter = sbuf([P, V], F32, "quarter")
-        ones = sbuf([P, V // 2], F32, "ones")
+        ones = sbuf([P, V], F32, "ones")
         nc.vector.memset(ones[:], 1.0)
-        nc.scalar.mul(quarter[:, : V // 2], ones[:], 0.25)
+        nc.scalar.mul(quarter[:], ones[:], 0.25)
 
         w1_raw = sbuf([P, PACK, H], F32, "w1_raw")
         nc.sync.dma_start(w1_raw[:], w1.rearrange("(p j) c -> p j c", j=PACK))
@@ -60,12 +60,9 @@ def tile_picked_ydcons_relu_po_kernel(
         nc.vector.tensor_copy(x_scale_rows[:], x_scale_table[:].indirect(offs_sb[:]))
         for q in range(4):
             lo = P - SCALE_ROWS + 4 * q
-            nc.scalar.dma_start(
+            nc.sync.dma_start(
                 x_scales_picked[32 * q : 32 * q + 4, :].bitcast(I32), x_scale_rows[lo : lo + 4, :].bitcast(I32)
             )
-        late_ones = sbuf([P, V // 2], F32, "late_ones", "x_scale_table")
-        nc.vector.memset(late_ones[:], 1.0)
-        nc.scalar.mul(quarter[:, V // 2 :], late_ones[:], 0.25)
 
         def deal_views(raw, name, t_lo, t_hi, tag=None):
             nt = t_hi - t_lo

@@ -45,9 +45,13 @@ def tile_picked_ydcons_relu_po_kernel(
         x_scales_picked = sbuf([P, S], U8, "x_scales_picked")
         nc.vector.memset(x_scales_picked[:].bitcast(I32), 0)
         quarter = sbuf([P, V], F32, "quarter")
-        ones = sbuf([P, V], F32, "ones")
+        ones = sbuf([P, V // 2], F32, "ones")
         nc.vector.memset(ones[:], 1.0)
-        nc.scalar.mul(quarter[:], ones[:], 0.25)
+        nc.scalar.mul(quarter[:, : V // 2], ones[:], 0.25)
+        one = sbuf([P, 1], F32, "one")
+        nc.vector.memset(one[:], 1.0)
+        early_half = sbuf([P, V // 2], F32, "early_half")
+        nc.vector.memset(early_half[:], 0.5)
 
         w1_raw = sbuf([P, PACK, H], F32, "w1_raw")
         nc.sync.dma_start(w1_raw[:], w1.rearrange("(p j) c -> p j c", j=PACK))
@@ -63,6 +67,10 @@ def tile_picked_ydcons_relu_po_kernel(
             nc.sync.dma_start(
                 x_scales_picked[32 * q : 32 * q + 4, :].bitcast(I32), x_scale_rows[lo : lo + 4, :].bitcast(I32)
             )
+
+        late_half = sbuf([P, V // 2], F32, "late_half", "x_scale_table")
+        nc.vector.memset(late_half[:], 0.5)
+        nc.vector.tensor_tensor(quarter[:, V // 2 :], early_half[:], late_half[:], ALU.mult)
 
         def deal_views(raw, name, t_lo, t_hi, tag=None):
             nt = t_hi - t_lo
@@ -93,13 +101,16 @@ def tile_picked_ydcons_relu_po_kernel(
         nc.vector.tensor_copy(dst[:, :W1_VECTOR_M], src[:, :W1_VECTOR_M])
         nc.scalar.copy(dst[:, W1_VECTOR_M:], src[:, W1_VECTOR_M:])
         w1_q = quantize(w1_bf16[:], "w1")
-        w2_raw = sbuf([P, PACK, N], F32, "w2_raw", "x_scale_table")
-        nc.sync.dma_start(w2_raw[:], w2.rearrange("(p j) c -> p j c", j=PACK))
+        half = S // 2
+        w2_halves = [
+            sbuf([P, PACK * N // 2], F32, "w2_raw%d" % u, tag)[:] for u, tag in enumerate(("x_scale_table", "early_half"))
+        ]
+        w2_rows = w2.rearrange("(p j) c -> p j c", j=PACK)
+        for u in range(2):
+            nc.sync.dma_start(w2_halves[u].rearrange("p (j c) -> p j c", j=PACK), w2_rows[:, :, u * N // 2 : (u + 1) * N // 2])
         meas_raw = sbuf([P, PACK, V], F32, "meas_raw", "x_scale_rows")
         nc.sync.dma_start(meas_raw[:], meas.rearrange("(p t) v -> p t v", t=PACK))
 
-
-        half = S // 2
         x_picked = sbuf([P, S], U32, "x_picked", "w1_bf16")
         for lo, hi in ((0, CHUNK), (CHUNK, half), (half, S)):
             nc.vector.tensor_copy(x_picked[:, lo:hi], x_word_table[:].indirect(offs_sb[:, lo // 16 : hi // 16]))
@@ -124,46 +135,57 @@ def tile_picked_ydcons_relu_po_kernel(
             src = h_banks[c][:].rearrange("p t n -> p n t")
             nc.scalar.activation(dst, src, ACT.Relu)
 
-        w2_low, dst_low, src_low = deal_views(w2_raw, "w2_low", 0, 2)
-        w2_high, dst_high, src_high = deal_views(w2_raw, "w2_high", 2, PACK)
-        h_scales = sbuf([P, S], U8, "h_scales")
+        w2_bf16 = sbuf([P, PACK * P * PACK], BF16, "w2_bf16")
+        w2_dst = w2_bf16[:].rearrange("p (t m j) -> p m j t", t=PACK, j=PACK)
 
-        nc.vector.tensor_copy(dst_low, src_low)
-        w2_q_low = quantize(w2_low[:], "w2_low")
-        h_codes = sbuf([P, S], U32, "h_codes", "w2_low_bf16")
-        for c in range(n_chunks):
-            cols = slice(c * CHUNK, (c + 1) * CHUNK)
-            nc.vector.quantize_mx(out=h_codes[:, cols].bitcast(FP8X4), scales=h_scales[:, cols], in_=h_bf16[c][:])
-        nc.vector.tensor_copy(dst_high[:, : P // 2], src_high[:, : P // 2])
-        nc.vector.tensor_copy(dst_high[:, P // 2 :], src_high[:, P // 2 :])
-        w2_q_high = quantize(w2_high[:], "w2_high")
+        def w2_views(u, t_lo, t_hi):
+            src = w2_halves[u].rearrange("p (j m t) -> p m j t", j=PACK, t=PACK)
+            return w2_dst[:, u * P // 2 : (u + 1) * P // 2, :, t_lo:t_hi], src[:, :, :, t_lo:t_hi]
+
+        def quantize_h(c):
+            codes, scales, cols = h_operand(c, c + 1)
+            nc.vector.quantize_mx(out=codes.bitcast(FP8X4), scales=scales, in_=h_bf16[c][:])
+
+        def h_operand(lo, hi):
+            codes, scales, first = h_parts[min(lo, 1)]
+            cols = slice((lo - first) * CHUNK, (hi - first) * CHUNK)
+            return codes[:, cols], scales[:, cols], slice(lo * CHUNK, hi * CHUNK)
+
+        nc.vector.tensor_copy(*w2_views(0, 0, PACK))
+        h_parts = [(sbuf([P, CHUNK], U32, "h_codes_first", "x_scale_table"), sbuf([P, CHUNK], U8, "h_scales_first"), 0)]
+        quantize_h(0)
+        nc.vector.tensor_scalar(*w2_views(1, 0, 2), one[:], None, ALU.mult)
+        h_parts.append(
+            (sbuf([P, S - CHUNK], U32, "h_codes_rest", "one"), sbuf([P, S - CHUNK], U8, "h_scales_rest"), 1)
+        )
+        quantize_h(1)
+        w2_q_low = quantize(w2_bf16[:, : 2 * P * PACK], "w2_low")
+        quantize_h(2)
+        quantize_h(3)
+        nc.vector.tensor_copy(*w2_views(1, 2, PACK))
 
         out_rows = out_0.rearrange("(p t) n -> p t n", t=PACK)
-        meas3 = sbuf([P, PACK, V], F32, "meas3")
-        nc.vector.tensor_scalar(meas3[:], meas_raw[:], 3.0, None, ALU.mult)
-        y_tiles = {}
+        meas3 = [sbuf([P, 2, V], F32, "meas3_low", "h_bf16_3"), sbuf([P, 2, V], F32, "meas3_high")]
+        nc.vector.tensor_scalar(meas3[0][:], meas_raw[:, :2], 3.0, None, ALU.mult)
+        nc.scalar.mul(meas3[1][:], meas_raw[:, 2:], 3.0)
+        w2_q_high = quantize(w2_bf16[:, 2 * P * PACK :], "w2_high")
 
-        def second_layer(t, engine_copy):
+        y_tiles = {t: sbuf([P, S], F32, "y%d" % t) for t in range(PACK)}
+
+        def second_layer(t, runs, bank_tag, engine_copy):
             weights = (w2_q_low, w2_q_high)[t // 2]
             w_cols = slice(t % 2 * P, (t % 2 + 1) * P)
-            y = sbuf([P, S], F32, "y%d" % t)
-            bank = ps.tile([P, S], F32, name="y_bank%d" % t, tag="y_bank%d" % t)
-            pieces = [(bank, 0, n_chunks)]
-            if t == 0:
-                late = [ps.tile([P, S], F32, name="y_late%d" % i, tag="h_bank%d" % i) for i in range(2)]
-                pieces = [(bank, 0, 2), (late[0], 2, 3), (late[1], 3, 4)]
-            if t == 1:
-                pieces = [(bank, 0, 2), (ps.tile([P, S], F32, name="y1_late", tag="h_bank2"), 2, 4)]
-            for piece, lo, hi in pieces:
-                cols = slice(lo * CHUNK, hi * CHUNK)
-                product(piece[:, cols], weights, w_cols, h_codes[:, cols], h_scales[:, cols])
-                engine_copy(y[:, cols], piece[:, cols])
-            y_tiles[t] = y
+            bank = ps.tile([P, S], F32, name="y_bank%d_%d" % (t, runs[0][0]), tag=bank_tag)
+            for lo, hi in runs:
+                codes, scales, cols = h_operand(lo, hi)
+                product(bank[:, cols], weights, w_cols, codes, scales)
+            cols = slice(runs[0][0] * CHUNK, runs[-1][1] * CHUNK)
+            engine_copy(y_tiles[t][:, cols], bank[:, cols])
 
         picked = [sbuf([P, V], F32, "picked%d" % t) for t in range(PACK)]
 
         def fetch(t):
-            nc.vector.tensor_tensor(picked[t][:], y_tiles[t][:].indirect(line_sb[:]), meas3[:, t, :], ALU.add)
+            nc.vector.tensor_tensor(picked[t][:], y_tiles[t][:].indirect(line_sb[:]), meas3[t // 2][:, t % 2, :], ALU.add)
 
         def put_back(t, on_vector):
             y = y_tiles[t]
@@ -177,11 +199,15 @@ def tile_picked_ydcons_relu_po_kernel(
             rows = pairs[:].rearrange("p (a n b) -> p a n b", a=2, b=2)
             engine_copy(rows[:, t // 2, lo:hi, t % 2], y_tiles[t][:, lo:hi])
 
-        second_layer(0, nc.scalar.copy)
-        second_layer(1, nc.scalar.copy)
-        second_layer(2, nc.scalar.copy)
+        all_runs = ((0, 1), (1, 3), (3, 4))
+        second_layer(0, all_runs[:1], "y_bank0", nc.scalar.copy)
+        second_layer(1, all_runs[:1], "y_bank1", nc.scalar.copy)
+        second_layer(0, all_runs[1:2], "h_bank0", nc.scalar.copy)
+        second_layer(0, all_runs[2:], "h_bank1", nc.scalar.copy)
+        second_layer(1, all_runs[1:], "h_bank2", nc.scalar.copy)
+        second_layer(2, all_runs, "y_bank2", nc.scalar.copy)
         fetch(0)
-        second_layer(3, nc.vector.tensor_copy)
+        second_layer(3, all_runs, "h_bank1", nc.vector.tensor_copy)
         fetch(1)
         fetch(3)
         fetch(2)
@@ -193,7 +219,7 @@ def tile_picked_ydcons_relu_po_kernel(
         out_codes = sbuf([P, S], U32, "out_codes")
         out_scales = sbuf([P, S], U8, "out_scales")
         out_words = out_1[0].rearrange("p n t -> p (n t)").bitcast(I32)
-        pairs = sbuf([P, 2 * S * 2], BF16, "pairs", "meas3")
+        pairs = sbuf([P, 2 * S * 2], BF16, "pairs", "meas3_high")
         round_rows(0, 0, S, nc.vector.tensor_copy)
         round_rows(1, 0, S, nc.vector.tensor_copy)
         round_rows(3, 0, VECTOR_COLS, nc.vector.tensor_copy)

@@ -41,17 +41,15 @@ def tile_picked_ydcons_relu_po_kernel(
         x_scale_table = sbuf([P, T], U8, "x_scale_table")
         nc.scalar.dma_start(x_scale_table[P - SCALE_ROWS :, :].bitcast(I32), x_scales[0].bitcast(I32))
         nc.sync.dma_start(offs_sb[:], offs)
-        nc.vector.memset(x_scale_table[: P - SCALE_ROWS, :].bitcast(I32), 0)
+        nc.gpsimd.memset(x_scale_table[: P - SCALE_ROWS, :].bitcast(I32), 0)
         x_scales_picked = sbuf([P, S], U8, "x_scales_picked")
-        nc.vector.memset(x_scales_picked[:].bitcast(I32), 0)
+        nc.gpsimd.memset(x_scales_picked[:].bitcast(I32), 0)
         quarter = sbuf([P, V], F32, "quarter")
         ones = sbuf([P, V // 2], F32, "ones")
-        nc.vector.memset(ones[:], 1.0)
+        nc.gpsimd.memset(ones[:], 1.0)
         nc.scalar.mul(quarter[:, : V // 2], ones[:], 0.25)
-        one = sbuf([P, 1], F32, "one")
-        nc.vector.memset(one[:], 1.0)
-        early_half = sbuf([P, V // 2], F32, "early_half")
-        nc.vector.memset(early_half[:], 0.5)
+        early_half = sbuf([P, 1], F32, "early_half")
+        nc.gpsimd.memset(early_half[:], 0.5)
 
         w1_raw = sbuf([P, PACK, H], F32, "w1_raw")
         nc.sync.dma_start(w1_raw[:], w1.rearrange("(p j) c -> p j c", j=PACK))
@@ -69,8 +67,8 @@ def tile_picked_ydcons_relu_po_kernel(
             )
 
         late_half = sbuf([P, V // 2], F32, "late_half", "x_scale_table")
-        nc.vector.memset(late_half[:], 0.5)
-        nc.vector.tensor_tensor(quarter[:, V // 2 :], early_half[:], late_half[:], ALU.mult)
+        nc.gpsimd.memset(late_half[:], 0.5)
+        nc.scalar.activation(quarter[:, V // 2 :], late_half[:], ACT.Copy, scale=early_half[:])
 
         def deal_views(raw, name, t_lo, t_hi, tag=None):
             nt = t_hi - t_lo
@@ -108,7 +106,7 @@ def tile_picked_ydcons_relu_po_kernel(
         w2_rows = w2.rearrange("(p j) c -> p j c", j=PACK)
         for u in range(2):
             nc.sync.dma_start(w2_halves[u].rearrange("p (j c) -> p j c", j=PACK), w2_rows[:, :, u * N // 2 : (u + 1) * N // 2])
-        meas_raw = sbuf([P, PACK, V], F32, "meas_raw", "x_scale_rows")
+        meas_raw = sbuf([P, PACK, V], F32, "meas_raw", "w1_raw")
         nc.sync.dma_start(meas_raw[:], meas.rearrange("(p t) v -> p t v", t=PACK))
 
         x_picked = sbuf([P, S], U32, "x_picked", "w1_bf16")
@@ -129,11 +127,13 @@ def tile_picked_ydcons_relu_po_kernel(
                 )
             h_banks.append(bank)
 
-        h_bf16 = [sbuf([P, CHUNK * PACK], BF16, "h_bf16_%d" % c) for c in range(n_chunks)]
-        for c in range(n_chunks):
-            dst = h_bf16[c][:].rearrange("p (n t) -> p n t", t=PACK)
-            src = h_banks[c][:].rearrange("p t n -> p n t")
-            nc.scalar.activation(dst, src, ACT.Relu)
+        all_runs = ((0, 1), (1, 3), (3, 4))
+        h_bf16 = [sbuf([P, (hi - lo) * CHUNK * PACK], BF16, "h_bf16_%d" % lo) for lo, hi in all_runs]
+        for values, (lo, hi) in zip(h_bf16, all_runs):
+            for c in range(lo, hi):
+                dst = values[:, (c - lo) * CHUNK * PACK : (c - lo + 1) * CHUNK * PACK]
+                src = h_banks[c][:].rearrange("p t n -> p n t")
+                nc.scalar.activation(dst.rearrange("p (n t) -> p n t", t=PACK), src, ACT.Relu)
 
         w2_bf16 = sbuf([P, PACK * P * PACK], BF16, "w2_bf16")
         w2_dst = w2_bf16[:].rearrange("p (t m j) -> p m j t", t=PACK, j=PACK)
@@ -142,9 +142,9 @@ def tile_picked_ydcons_relu_po_kernel(
             src = w2_halves[u].rearrange("p (j m t) -> p m j t", j=PACK, t=PACK)
             return w2_dst[:, u * P // 2 : (u + 1) * P // 2, :, t_lo:t_hi], src[:, :, :, t_lo:t_hi]
 
-        def quantize_h(c):
-            codes, scales, cols = h_operand(c, c + 1)
-            nc.vector.quantize_mx(out=codes.bitcast(FP8X4), scales=scales, in_=h_bf16[c][:])
+        def quantize_h(i):
+            codes, scales, cols = h_operand(*all_runs[i])
+            nc.vector.quantize_mx(out=codes.bitcast(FP8X4), scales=scales, in_=h_bf16[i][:])
 
         def h_operand(lo, hi):
             codes, scales, first = h_parts[min(lo, 1)]
@@ -154,21 +154,20 @@ def tile_picked_ydcons_relu_po_kernel(
         nc.vector.tensor_copy(*w2_views(0, 0, PACK))
         h_parts = [(sbuf([P, CHUNK], U32, "h_codes_first", "x_scale_table"), sbuf([P, CHUNK], U8, "h_scales_first"), 0)]
         quantize_h(0)
-        nc.vector.tensor_scalar(*w2_views(1, 0, 2), one[:], None, ALU.mult)
+        nc.vector.tensor_copy(*w2_views(1, 0, 2))
         h_parts.append(
-            (sbuf([P, S - CHUNK], U32, "h_codes_rest", "one"), sbuf([P, S - CHUNK], U8, "h_scales_rest"), 1)
+            (sbuf([P, S - CHUNK], U32, "h_codes_rest", "early_half"), sbuf([P, S - CHUNK], U8, "h_scales_rest"), 1)
         )
-        quantize_h(1)
-        w2_q_low = quantize(w2_bf16[:, : 2 * P * PACK], "w2_low")
-        quantize_h(2)
-        quantize_h(3)
         nc.vector.tensor_copy(*w2_views(1, 2, PACK))
+        w2_q_low = quantize(w2_bf16[:, : 2 * P * PACK], "w2_low")
+        quantize_h(1)
+        quantize_h(2)
 
         out_rows = out_0.rearrange("(p t) n -> p t n", t=PACK)
-        meas3 = [sbuf([P, 2, V], F32, "meas3_low", "h_bf16_3"), sbuf([P, 2, V], F32, "meas3_high")]
-        nc.vector.tensor_scalar(meas3[0][:], meas_raw[:, :2], 3.0, None, ALU.mult)
-        nc.scalar.mul(meas3[1][:], meas_raw[:, 2:], 3.0)
         w2_q_high = quantize(w2_bf16[:, 2 * P * PACK :], "w2_high")
+        meas3 = sbuf([P, PACK, V], F32, "meas3", "h_bf16_3")
+        nc.vector.tensor_scalar(meas3[:, :2], meas_raw[:, :2], 3.0, None, ALU.mult)
+        nc.vector.tensor_scalar(meas3[:, 2:], meas_raw[:, 2:], 3.0, None, ALU.mult)
 
         y_tiles = {t: sbuf([P, S], F32, "y%d" % t) for t in range(PACK)}
 
@@ -185,7 +184,7 @@ def tile_picked_ydcons_relu_po_kernel(
         picked = [sbuf([P, V], F32, "picked%d" % t) for t in range(PACK)]
 
         def fetch(t):
-            nc.vector.tensor_tensor(picked[t][:], y_tiles[t][:].indirect(line_sb[:]), meas3[t // 2][:, t % 2, :], ALU.add)
+            nc.vector.tensor_tensor(picked[t][:], y_tiles[t][:].indirect(line_sb[:]), meas3[:, t, :], ALU.add)
 
         def put_back(t, on_vector):
             y = y_tiles[t]
@@ -199,7 +198,6 @@ def tile_picked_ydcons_relu_po_kernel(
             rows = pairs[:].rearrange("p (a n b) -> p a n b", a=2, b=2)
             engine_copy(rows[:, t // 2, lo:hi, t % 2], y_tiles[t][:, lo:hi])
 
-        all_runs = ((0, 1), (1, 3), (3, 4))
         second_layer(0, all_runs[:1], "y_bank0", nc.scalar.copy)
         second_layer(1, all_runs[:1], "y_bank1", nc.scalar.copy)
         second_layer(0, all_runs[1:2], "h_bank0", nc.scalar.copy)
@@ -209,24 +207,24 @@ def tile_picked_ydcons_relu_po_kernel(
         fetch(0)
         second_layer(3, all_runs, "h_bank1", nc.vector.tensor_copy)
         fetch(1)
-        fetch(3)
         fetch(2)
+        fetch(3)
         put_back(0, False)
         put_back(1, False)
-        put_back(2, False)
-        put_back(3, True)
+        put_back(3, False)
+        put_back(2, True)
         halves = [slice(u * half, (u + 1) * half) for u in range(2)]
         out_codes = sbuf([P, S], U32, "out_codes")
         out_scales = sbuf([P, S], U8, "out_scales")
         out_words = out_1[0].rearrange("p n t -> p (n t)").bitcast(I32)
-        pairs = sbuf([P, 2 * S * 2], BF16, "pairs", "meas3_high")
+        pairs = sbuf([P, 2 * S * 2], BF16, "pairs", "h_bf16_3")
         round_rows(0, 0, S, nc.vector.tensor_copy)
         round_rows(1, 0, S, nc.vector.tensor_copy)
-        round_rows(3, 0, VECTOR_COLS, nc.vector.tensor_copy)
-        round_rows(2, 0, half, nc.vector.tensor_copy)
-        round_rows(2, half, VECTOR_COLS, nc.vector.tensor_copy)
-        round_rows(3, VECTOR_COLS, S, nc.scalar.copy)
+        round_rows(2, 0, VECTOR_COLS, nc.vector.tensor_copy)
+        round_rows(3, 0, half, nc.vector.tensor_copy)
+        round_rows(3, half, VECTOR_COLS, nc.vector.tensor_copy)
         round_rows(2, VECTOR_COLS, S, nc.scalar.copy)
+        round_rows(3, VECTOR_COLS, S, nc.scalar.copy)
         out_bf16 = [sbuf([P, half * PACK], BF16, "out_bf16_%d" % u) for u in range(2)]
 
         def weave(lo, hi, engine_copy, dtype):

@@ -18,9 +18,11 @@ ACT = mybir.ActivationFunctionType
 P = 128
 PACK = 4
 CHUNK = 128
+EARLY = S - CHUNK
 SCALE_ROWS = 16
 W1_VECTOR_M = 84
 VECTOR_COLS = 384
+SHARED = 64
 
 
 def tile_picked_ydcons_relu_po_kernel(
@@ -30,6 +32,7 @@ def tile_picked_ydcons_relu_po_kernel(
     with ExitStack() as ctx:
         lists = ctx.enter_context(tc.tile_pool(name="lists", bufs=1))
         sb = ctx.enter_context(tc.tile_pool(name="sb", bufs=1))
+        placed = ctx.enter_context(tc.tile_pool(name="placed", bufs=1))
         ps = ctx.enter_context(tc.psum_pool(name="ps", bufs=1))
 
         offs_sb = lists.tile([P, S // 16], U16, name="offs_sb")
@@ -38,18 +41,20 @@ def tile_picked_ydcons_relu_po_kernel(
         def sbuf(shape, dtype, name, tag=None):
             return sb.tile(shape, dtype, name=name, tag=tag or name, align_bytes=64)
 
-        x_scale_table = sbuf([P, T], U8, "x_scale_table")
+        def placed_at(offset, shape, dtype, name):
+            return placed.tile(shape, dtype, name=name, align_bytes=64, offset=offset)
+
+        half_bytes = PACK * N // 2 * 4
+        x_scale_table = placed_at(half_bytes - T // 2, [P, T], U8, "x_scale_table")
         nc.scalar.dma_start(x_scale_table[P - SCALE_ROWS :, :].bitcast(I32), x_scales[0].bitcast(I32))
         nc.sync.dma_start(offs_sb[:], offs)
         nc.gpsimd.memset(x_scale_table[: P - SCALE_ROWS, :].bitcast(I32), 0)
         x_scales_picked = sbuf([P, S], U8, "x_scales_picked")
         nc.gpsimd.memset(x_scales_picked[:].bitcast(I32), 0)
-        quarter = sbuf([P, V], F32, "quarter")
-        ones = sbuf([P, V // 2], F32, "ones")
+        ones = sbuf([P, V], F32, "ones")
         nc.gpsimd.memset(ones[:], 1.0)
-        nc.scalar.mul(quarter[:, : V // 2], ones[:], 0.25)
-        early_half = sbuf([P, 1], F32, "early_half")
-        nc.gpsimd.memset(early_half[:], 0.5)
+        quarter = sbuf([P, V], F32, "quarter")
+        nc.scalar.mul(quarter[:], ones[:], 0.25)
 
         w1_raw = sbuf([P, PACK, H], F32, "w1_raw")
         nc.sync.dma_start(w1_raw[:], w1.rearrange("(p j) c -> p j c", j=PACK))
@@ -65,21 +70,16 @@ def tile_picked_ydcons_relu_po_kernel(
             nc.sync.dma_start(
                 x_scales_picked[32 * q : 32 * q + 4, :].bitcast(I32), x_scale_rows[lo : lo + 4, :].bitcast(I32)
             )
+        w2_rows = w2.rearrange("(p j) c -> p j c", j=PACK)
+        w2_halves = [placed_at(u * half_bytes, [P, PACK * N // 2], F32, "w2_raw%d" % u) for u in range(2)]
+        for u in range(2):
+            nc.sync.dma_start(
+                w2_halves[u][:].rearrange("p (j c) -> p j c", j=PACK), w2_rows[:, :, u * N // 2 : (u + 1) * N // 2]
+            )
 
-        late_half = sbuf([P, V // 2], F32, "late_half", "x_scale_table")
-        nc.gpsimd.memset(late_half[:], 0.5)
-        nc.scalar.activation(quarter[:, V // 2 :], late_half[:], ACT.Copy, scale=early_half[:])
-
-        def deal_views(raw, name, t_lo, t_hi, tag=None):
-            nt = t_hi - t_lo
-            dealt = sbuf([P, nt * P * PACK], BF16, name + "_bf16", tag)
-            dst = dealt[:].rearrange("p (t m j) -> p m j t", t=nt, j=PACK)
-            src = raw[:].rearrange("p j (m t) -> p m j t", t=PACK)[:, :, :, t_lo:t_hi]
-            return dealt, dst, src
-
-        def quantize(values, name, tag=None):
+        def quantize(values, name):
             width = values.shape[1] // PACK
-            codes = sbuf([P, width], U32, name + "_codes", tag)
+            codes = sbuf([P, width], U32, name + "_codes")
             scales = sbuf([P, width], U8, name + "_scales")
             nc.vector.quantize_mx(out=codes[:].bitcast(FP8X4), scales=scales[:], in_=values)
             return codes, scales
@@ -95,151 +95,140 @@ def tile_picked_ydcons_relu_po_kernel(
                 stop=True,
             )
 
-        w1_bf16, dst, src = deal_views(w1_raw, "w1", 0, PACK)
+        w1_bf16 = sbuf([P, PACK * H], BF16, "w1_bf16")
+        dst = w1_bf16[:].rearrange("p (t m j) -> p m j t", t=PACK, j=PACK)
+        src = w1_raw[:].rearrange("p j (m t) -> p m j t", t=PACK)
         nc.vector.tensor_copy(dst[:, :W1_VECTOR_M], src[:, :W1_VECTOR_M])
         nc.scalar.copy(dst[:, W1_VECTOR_M:], src[:, W1_VECTOR_M:])
         w1_q = quantize(w1_bf16[:], "w1")
-        half = S // 2
-        w2_halves = [
-            sbuf([P, PACK * N // 2], F32, "w2_raw%d" % u, tag)[:] for u, tag in enumerate(("x_scale_table", "early_half"))
-        ]
-        w2_rows = w2.rearrange("(p j) c -> p j c", j=PACK)
-        for u in range(2):
-            nc.sync.dma_start(w2_halves[u].rearrange("p (j c) -> p j c", j=PACK), w2_rows[:, :, u * N // 2 : (u + 1) * N // 2])
-        meas_raw = sbuf([P, PACK, V], F32, "meas_raw", "w1_raw")
-        nc.sync.dma_start(meas_raw[:], meas.rearrange("(p t) v -> p t v", t=PACK))
+        meas_raw = sbuf([P, PACK * V], F32, "meas_raw", "w1_raw")
+        nc.sync.dma_start(meas_raw[:], meas.rearrange("(p t) v -> p (t v)", t=PACK))
 
+        half = S // 2
         x_picked = sbuf([P, S], U32, "x_picked", "w1_bf16")
         for lo, hi in ((0, CHUNK), (CHUNK, half), (half, S)):
             nc.vector.tensor_copy(x_picked[:, lo:hi], x_word_table[:].indirect(offs_sb[:, lo // 16 : hi // 16]))
 
-        n_chunks = S // CHUNK
-        h_banks = []
-        for c in range(n_chunks):
-            bank = ps.tile([P, PACK, CHUNK], F32, name="h_bank%d" % c)
-            for t in range(PACK):
-                product(
-                    bank[:, t, :],
-                    w1_q,
-                    slice(t * P, (t + 1) * P),
-                    x_picked[:, c * CHUNK : (c + 1) * CHUNK],
-                    x_scales_picked[:, c * CHUNK : (c + 1) * CHUNK],
+        runs = ((0, CHUNK), (CHUNK, EARLY), (EARLY, S))
+        h_bf16 = [sbuf([P, (hi - lo) * PACK], BF16, "h_bf16_%d" % i) for i, (lo, hi) in enumerate(runs)]
+        for values, (lo, hi) in zip(h_bf16, runs):
+            for first in range(lo, hi, CHUNK):
+                bank = ps.tile([P, PACK, CHUNK], F32, name="h_bank%d" % (first // CHUNK))
+                cols = slice(first, first + CHUNK)
+                for t in range(PACK):
+                    product(bank[:, t, :], w1_q, slice(t * P, (t + 1) * P), x_picked[:, cols], x_scales_picked[:, cols])
+                dst = values[:, (first - lo) * PACK : (first - lo + CHUNK) * PACK]
+                nc.scalar.activation(
+                    dst.rearrange("p (n t) -> p n t", t=PACK), bank[:].rearrange("p t n -> p n t"), ACT.Relu
                 )
-            h_banks.append(bank)
 
-        all_runs = ((0, 1), (1, 3), (3, 4))
-        h_bf16 = [sbuf([P, (hi - lo) * CHUNK * PACK], BF16, "h_bf16_%d" % lo) for lo, hi in all_runs]
-        for values, (lo, hi) in zip(h_bf16, all_runs):
-            for c in range(lo, hi):
-                dst = values[:, (c - lo) * CHUNK * PACK : (c - lo + 1) * CHUNK * PACK]
-                src = h_banks[c][:].rearrange("p t n -> p n t")
-                nc.scalar.activation(dst.rearrange("p (n t) -> p n t", t=PACK), src, ACT.Relu)
-
-        w2_bf16 = sbuf([P, PACK * P * PACK], BF16, "w2_bf16")
+        w2_bf16 = sbuf([P, PACK * N], BF16, "w2_bf16")
         w2_dst = w2_bf16[:].rearrange("p (t m j) -> p m j t", t=PACK, j=PACK)
 
-        def w2_views(u, t_lo, t_hi):
-            src = w2_halves[u].rearrange("p (j m t) -> p m j t", j=PACK, t=PACK)
-            return w2_dst[:, u * P // 2 : (u + 1) * P // 2, :, t_lo:t_hi], src[:, :, :, t_lo:t_hi]
+        def deal_w2(u, t_lo, t_hi):
+            src = w2_halves[u][:].rearrange("p (j m t) -> p m j t", j=PACK, t=PACK)
+            nc.vector.tensor_copy(
+                w2_dst[:, u * P // 2 : (u + 1) * P // 2, :, t_lo:t_hi], src[:, :, :, t_lo:t_hi]
+            )
 
-        def quantize_h(i):
-            codes, scales, cols = h_operand(*all_runs[i])
-            nc.vector.quantize_mx(out=codes.bitcast(FP8X4), scales=scales, in_=h_bf16[i][:])
+        h_q = []
 
-        def h_operand(lo, hi):
-            codes, scales, first = h_parts[min(lo, 1)]
-            cols = slice((lo - first) * CHUNK, (hi - first) * CHUNK)
-            return codes[:, cols], scales[:, cols], slice(lo * CHUNK, hi * CHUNK)
+        def quantize_h(i, offset):
+            lo, hi = runs[i]
+            codes = placed_at(offset, [P, hi - lo], U32, "h_codes%d" % i)
+            scales = sbuf([P, hi - lo], U8, "h_scales%d" % i)
+            nc.vector.quantize_mx(out=codes[:].bitcast(FP8X4), scales=scales[:], in_=h_bf16[i][:])
+            h_q.append((codes, scales))
 
-        nc.vector.tensor_copy(*w2_views(0, 0, PACK))
-        h_parts = [(sbuf([P, CHUNK], U32, "h_codes_first", "x_scale_table"), sbuf([P, CHUNK], U8, "h_scales_first"), 0)]
-        quantize_h(0)
-        nc.vector.tensor_copy(*w2_views(1, 0, 2))
-        h_parts.append(
-            (sbuf([P, S - CHUNK], U32, "h_codes_rest", "early_half"), sbuf([P, S - CHUNK], U8, "h_scales_rest"), 1)
-        )
-        nc.vector.tensor_copy(*w2_views(1, 2, PACK))
-        w2_q_low = quantize(w2_bf16[:, : 2 * P * PACK], "w2_low")
-        quantize_h(1)
-        quantize_h(2)
+        y_tiles = [sbuf([P, S], F32, "y%d" % t) for t in range(PACK)]
 
-        out_rows = out_0.rearrange("(p t) n -> p t n", t=PACK)
-        w2_q_high = quantize(w2_bf16[:, 2 * P * PACK :], "w2_high")
-        meas3 = sbuf([P, PACK, V], F32, "meas3", "h_bf16_3")
-        nc.vector.tensor_scalar(meas3[:, :2], meas_raw[:, :2], 3.0, None, ALU.mult)
-        nc.vector.tensor_scalar(meas3[:, 2:], meas_raw[:, 2:], 3.0, None, ALU.mult)
-
-        y_tiles = {t: sbuf([P, S], F32, "y%d" % t) for t in range(PACK)}
-
-        def second_layer(t, runs, bank_tag, engine_copy):
-            weights = (w2_q_low, w2_q_high)[t // 2]
+        def second_layer(t, lo, hi, bank_tag, engine_copy):
+            weights = w2_q[t // 2]
             w_cols = slice(t % 2 * P, (t % 2 + 1) * P)
-            bank = ps.tile([P, S], F32, name="y_bank%d_%d" % (t, runs[0][0]), tag=bank_tag)
-            for lo, hi in runs:
-                codes, scales, cols = h_operand(lo, hi)
-                product(bank[:, cols], weights, w_cols, codes, scales)
-            cols = slice(runs[0][0] * CHUNK, runs[-1][1] * CHUNK)
-            engine_copy(y_tiles[t][:, cols], bank[:, cols])
+            bank = ps.tile([P, S], F32, name="y_bank%d_%d" % (t, lo), tag=bank_tag)
+            for (codes, scales), (first, last) in zip(h_q, runs):
+                a, b = max(lo, first), min(hi, last)
+                if a < b:
+                    part = slice(a - first, b - first)
+                    product(bank[:, a:b], weights, w_cols, codes[:, part], scales[:, part])
+            engine_copy(y_tiles[t][:, lo:hi], bank[:, lo:hi])
+
+        deal_w2(0, 0, PACK)
+        deal_w2(1, 0, PACK)
+        quantize_h(0, half_bytes + 4 * EARLY)
+        w2_q = [quantize(w2_bf16[:, : 2 * P * PACK], "w2_low")]
+        quantize_h(1, half_bytes)
+        quantize_h(2, half_bytes + 4 * half)
+        w2_q.append(quantize(w2_bf16[:, 2 * P * PACK :], "w2_high"))
+
+        meas3 = sbuf([P, PACK * V], F32, "meas3", "h_bf16_2")
+        for u in range(2):
+            cols = slice(2 * u * V, 2 * (u + 1) * V)
+            nc.vector.tensor_scalar(meas3[:, cols], meas_raw[:, cols], 3.0, None, ALU.mult)
+
+        second_layer(0, 0, CHUNK, "y_bank0", nc.scalar.copy)
+        second_layer(1, 0, CHUNK, "y_bank1", nc.scalar.copy)
+        second_layer(0, CHUNK, EARLY, "h_bank0", nc.scalar.copy)
+        second_layer(0, EARLY, S, "h_bank1", nc.scalar.copy)
+        second_layer(1, CHUNK, S, "h_bank2", nc.scalar.copy)
+        second_layer(2, 0, S, "y_bank2", nc.scalar.copy)
+        second_layer(3, 0, half, "h_bank1", nc.vector.tensor_copy)
+        second_layer(3, half, S, "y_bank0", nc.scalar.copy)
 
         picked = [sbuf([P, V], F32, "picked%d" % t) for t in range(PACK)]
+        for t in range(PACK):
+            nc.vector.tensor_tensor(
+                picked[t][:], y_tiles[t][:].indirect(line_sb[:]), meas3[:, t * V : (t + 1) * V], ALU.add
+            )
+        out_rows = out_0.rearrange("(p t) n -> p t n", t=PACK)
 
-        def fetch(t):
-            nc.vector.tensor_tensor(picked[t][:], y_tiles[t][:].indirect(line_sb[:]), meas3[:, t, :], ALU.add)
-
-        def put_back(t, on_vector):
-            y = y_tiles[t]
+        def put_back(t, lo, hi, on_vector):
+            target = y_tiles[t][:].indirect(line_sb[:, lo // 16 : hi // 16])
             if on_vector:
-                nc.vector.tensor_tensor(y[:].indirect(line_sb[:]), picked[t][:], quarter[:], ALU.mult)
+                nc.vector.tensor_tensor(target, picked[t][:, lo:hi], quarter[:, lo:hi], ALU.mult)
             else:
-                nc.scalar.activation(y[:].indirect(line_sb[:]), picked[t][:], ACT.Copy, scale=0.25)
-            nc.sync.dma_start(out_rows[:, t, :], y[:])
+                nc.scalar.activation(target, picked[t][:, lo:hi], ACT.Copy, scale=0.25)
+            if hi == V:
+                nc.sync.dma_start(out_rows[:, t, :], y_tiles[t][:])
+
+        put_back(0, 0, V, False)
+        put_back(1, 0, V, False)
+        put_back(2, 0, SHARED, True)
+        put_back(3, 0, V, True)
+        put_back(2, SHARED, V, False)
+
+        pairs = sbuf([P, 2 * S * 2], BF16, "pairs", "h_bf16_2")
 
         def round_rows(t, lo, hi, engine_copy):
             rows = pairs[:].rearrange("p (a n b) -> p a n b", a=2, b=2)
             engine_copy(rows[:, t // 2, lo:hi, t % 2], y_tiles[t][:, lo:hi])
 
-        second_layer(0, all_runs[:1], "y_bank0", nc.scalar.copy)
-        second_layer(1, all_runs[:1], "y_bank1", nc.scalar.copy)
-        second_layer(0, all_runs[1:2], "h_bank0", nc.scalar.copy)
-        second_layer(0, all_runs[2:], "h_bank1", nc.scalar.copy)
-        second_layer(1, all_runs[1:], "h_bank2", nc.scalar.copy)
-        second_layer(2, all_runs, "y_bank2", nc.scalar.copy)
-        fetch(0)
-        second_layer(3, all_runs, "h_bank1", nc.vector.tensor_copy)
-        fetch(1)
-        fetch(2)
-        fetch(3)
-        put_back(0, False)
-        put_back(1, False)
-        put_back(3, False)
-        put_back(2, True)
-        halves = [slice(u * half, (u + 1) * half) for u in range(2)]
-        out_codes = sbuf([P, S], U32, "out_codes")
-        out_scales = sbuf([P, S], U8, "out_scales")
-        out_words = out_1[0].rearrange("p n t -> p (n t)").bitcast(I32)
-        pairs = sbuf([P, 2 * S * 2], BF16, "pairs", "h_bf16_3")
         round_rows(0, 0, S, nc.vector.tensor_copy)
         round_rows(1, 0, S, nc.vector.tensor_copy)
-        round_rows(2, 0, VECTOR_COLS, nc.vector.tensor_copy)
-        round_rows(3, 0, half, nc.vector.tensor_copy)
-        round_rows(3, half, VECTOR_COLS, nc.vector.tensor_copy)
-        round_rows(2, VECTOR_COLS, S, nc.scalar.copy)
+        round_rows(3, 0, VECTOR_COLS, nc.vector.tensor_copy)
+        pieces = ((0, CHUNK), (CHUNK, VECTOR_COLS), (VECTOR_COLS, S))
+        for lo, hi in pieces[:2]:
+            round_rows(2, lo, hi, nc.vector.tensor_copy)
         round_rows(3, VECTOR_COLS, S, nc.scalar.copy)
-        out_bf16 = [sbuf([P, half * PACK], BF16, "out_bf16_%d" % u) for u in range(2)]
+        round_rows(2, VECTOR_COLS, S, nc.scalar.copy)
+        out_bf16 = [sbuf([P, (hi - lo) * PACK], BF16, "out_bf16_%d" % lo) for lo, hi in pieces]
 
-        def weave(lo, hi, engine_copy, dtype):
-            u = lo // half
-            words = out_bf16[u][:].bitcast(dtype)[:, 2 * (lo - u * half) : 2 * (hi - u * half)]
+        def weave(i, engine_copy, dtype):
+            lo, hi = pieces[i]
             engine_copy(
-                words.rearrange("p (n a) -> p n a", a=2),
+                out_bf16[i][:].bitcast(dtype).rearrange("p (n a) -> p n a", a=2),
                 pairs[:].bitcast(dtype).rearrange("p (a n) -> p n a", a=2)[:, lo:hi],
             )
 
-        weave(0, half, nc.vector.tensor_copy, I32)
-        weave(half, VECTOR_COLS, nc.vector.tensor_copy, I32)
-        weave(VECTOR_COLS, S, nc.scalar.copy, U32)
-        for u, cols in enumerate(halves):
-            nc.vector.quantize_mx(out=out_codes[:, cols].bitcast(FP8X4), scales=out_scales[:, cols], in_=out_bf16[u][:])
+        weave(0, nc.vector.tensor_copy, I32)
+        weave(1, nc.vector.tensor_copy, I32)
+        weave(2, nc.scalar.copy, U32)
+        out_codes = sbuf([P, S], U32, "out_codes")
+        out_scales = sbuf([P, S], U8, "out_scales")
+        out_words = out_1[0].rearrange("p n t -> p (n t)").bitcast(I32)
+        for values, (lo, hi) in zip(out_bf16, pieces):
+            nc.vector.quantize_mx(out=out_codes[:, lo:hi].bitcast(FP8X4), scales=out_scales[:, lo:hi], in_=values[:])
+        for cols in (slice(0, VECTOR_COLS), slice(VECTOR_COLS, S)):
             nc.sync.dma_start(out_words[:, cols], out_codes[:, cols].bitcast(I32))
         for q in range(4):
             queue = nc.scalar if q == 0 else nc.sync

@@ -23,6 +23,7 @@ SCALE_ROWS = 16
 W1_VECTOR_M = 84
 VECTOR_COLS = 384
 SHARED = 64
+W2_FIRST = 320
 
 
 def tile_picked_ydcons_relu_po_kernel(
@@ -44,7 +45,7 @@ def tile_picked_ydcons_relu_po_kernel(
         def placed_at(offset, shape, dtype, name):
             return placed.tile(shape, dtype, name=name, align_bytes=64, offset=offset)
 
-        half_bytes = PACK * N // 2 * 4
+        half_bytes = PACK * W2_FIRST * 4
         x_scale_table = placed_at(half_bytes - T // 2, [P, T], U8, "x_scale_table")
         nc.scalar.dma_start(x_scale_table[P - SCALE_ROWS :, :].bitcast(I32), x_scales[0].bitcast(I32))
         nc.sync.dma_start(offs_sb[:], offs)
@@ -71,11 +72,10 @@ def tile_picked_ydcons_relu_po_kernel(
                 x_scales_picked[32 * q : 32 * q + 4, :].bitcast(I32), x_scale_rows[lo : lo + 4, :].bitcast(I32)
             )
         w2_rows = w2.rearrange("(p j) c -> p j c", j=PACK)
-        w2_halves = [placed_at(u * half_bytes, [P, PACK * N // 2], F32, "w2_raw%d" % u) for u in range(2)]
-        for u in range(2):
-            nc.sync.dma_start(
-                w2_halves[u][:].rearrange("p (j c) -> p j c", j=PACK), w2_rows[:, :, u * N // 2 : (u + 1) * N // 2]
-            )
+        w2_cols = ((0, W2_FIRST), (W2_FIRST, N))
+        w2_halves = [placed_at(PACK * lo * 4, [P, PACK * (hi - lo)], F32, "w2_raw%d" % lo) for lo, hi in w2_cols]
+        for raw, (lo, hi) in zip(w2_halves, w2_cols):
+            nc.sync.dma_start(raw[:].rearrange("p (j c) -> p j c", j=PACK), w2_rows[:, :, lo:hi])
 
         def quantize(values, name):
             width = values.shape[1] // PACK
@@ -128,7 +128,7 @@ def tile_picked_ydcons_relu_po_kernel(
         def deal_w2(u, t_lo, t_hi):
             src = w2_halves[u][:].rearrange("p (j m t) -> p m j t", j=PACK, t=PACK)
             nc.vector.tensor_copy(
-                w2_dst[:, u * P // 2 : (u + 1) * P // 2, :, t_lo:t_hi], src[:, :, :, t_lo:t_hi]
+                w2_dst[:, w2_cols[u][0] // PACK : w2_cols[u][1] // PACK, :, t_lo:t_hi], src[:, :, :, t_lo:t_hi]
             )
 
         h_q = []
@@ -228,10 +228,9 @@ def tile_picked_ydcons_relu_po_kernel(
         out_words = out_1[0].rearrange("p n t -> p (n t)").bitcast(I32)
         for values, (lo, hi) in zip(out_bf16, pieces):
             nc.vector.quantize_mx(out=out_codes[:, lo:hi].bitcast(FP8X4), scales=out_scales[:, lo:hi], in_=values[:])
-        for cols in (slice(0, VECTOR_COLS), slice(VECTOR_COLS, S)):
-            nc.sync.dma_start(out_words[:, cols], out_codes[:, cols].bitcast(I32))
+            nc.sync.dma_start(out_words[:, lo:hi], out_codes[:, lo:hi].bitcast(I32))
         for q in range(4):
-            queue = nc.scalar if q == 0 else nc.sync
+            queue = nc.scalar if q < 2 else nc.sync
             queue.dma_start(
                 out_2[0, 4 * q : 4 * q + 4, :].bitcast(I32),
                 out_scales[32 * q : 32 * q + 4, :].bitcast(I32),

@@ -105,7 +105,7 @@ def tile_picked_ydcons_relu_po_kernel(
         nc.sync.dma_start(meas_raw[:], meas.rearrange("(p t) v -> p (t v)", t=PACK))
 
         half = S // 2
-        x_picked = sbuf([P, S], U32, "x_picked", "w1_bf16")
+        x_picked = placed_at(PACK * N * 4, [P, S], U32, "x_picked")
         for lo, hi in ((0, CHUNK), (CHUNK, half), (half, S)):
             nc.vector.tensor_copy(x_picked[:, lo:hi], x_word_table[:].indirect(offs_sb[:, lo // 16 : hi // 16]))
 

@@ -23,6 +23,9 @@ SCALE_ROWS = 16
 W1_VECTOR_M = 84
 VECTOR_COLS = 384
 SHARED = 64
+STRETCH = 32768
+STRETCH_START = 1024
+BYTES_OF = {F32: 4, U32: 4, BF16: 2, U8: 1}
 W2_FIRST = 320
 
 
@@ -33,38 +36,46 @@ def tile_picked_ydcons_relu_po_kernel(
     with ExitStack() as ctx:
         lists = ctx.enter_context(tc.tile_pool(name="lists", bufs=1))
         sb = ctx.enter_context(tc.tile_pool(name="sb", bufs=1))
-        placed = ctx.enter_context(tc.tile_pool(name="placed", bufs=1))
         ps = ctx.enter_context(tc.psum_pool(name="ps", bufs=1))
 
         offs_sb = lists.tile([P, S // 16], U16, name="offs_sb")
         line_sb = lists.tile([P, V // 16], U16, name="line_sb")
 
-        def sbuf(shape, dtype, name, tag=None):
-            return sb.tile(shape, dtype, name=name, tag=tag or name, align_bytes=64)
+        free = [r * STRETCH + STRETCH_START for r in range(7)]
+
+        def reserve(stretch, size):
+            at = free[stretch]
+            free[stretch] = at + size
+            return at
 
         def placed_at(offset, shape, dtype, name):
-            return placed.tile(shape, dtype, name=name, align_bytes=64, offset=offset)
+            return sb.tile(shape, dtype, name=name, align_bytes=64, offset=offset)
 
-        half_bytes = PACK * W2_FIRST * 4
-        x_scale_table = placed_at(half_bytes - T // 2, [P, T], U8, "x_scale_table")
+        def sbuf(stretch, columns, dtype, name):
+            return placed_at(reserve(stretch, columns * BYTES_OF[dtype]), [P, columns], dtype, name)
+
+        w2_at = reserve(3, PACK * N * 4)
+        w2_last_at = w2_at + PACK * W2_FIRST * 4
+        x_scale_table = placed_at(w2_last_at - T // 2, [P, T], U8, "x_scale_table")
         nc.scalar.dma_start(x_scale_table[P - SCALE_ROWS :, :].bitcast(I32), x_scales[0].bitcast(I32))
         nc.sync.dma_start(offs_sb[:], offs)
         nc.gpsimd.memset(x_scale_table[: P - SCALE_ROWS, :].bitcast(I32), 0)
-        x_scales_picked = sbuf([P, S], U8, "x_scales_picked")
+        x_scales_picked = sbuf(0, S, U8, "x_scales_picked")
         nc.gpsimd.memset(x_scales_picked[:].bitcast(I32), 0)
-        ones = sbuf([P, V], F32, "ones")
+        ones = sbuf(0, V, F32, "ones")
         nc.gpsimd.memset(ones[:], 1.0)
-        quarter = sbuf([P, V], F32, "quarter")
+        quarter = sbuf(0, V, F32, "quarter")
         nc.scalar.mul(quarter[:], ones[:], 0.25)
 
-        w1_raw = sbuf([P, PACK, H], F32, "w1_raw")
+        w1_at = reserve(0, PACK * H * 4)
+        w1_raw = placed_at(w1_at, [P, PACK, H], F32, "w1_raw")
         nc.sync.dma_start(w1_raw[:], w1.rearrange("(p j) c -> p j c", j=PACK))
-        x_word_table = sbuf([P, T], U32, "x_word_table")
+        x_word_table = sbuf(1, T, U32, "x_word_table")
         nc.sync.dma_start(
             x_word_table[:].bitcast(I32), x_words[0].rearrange("p n t -> p (n t)").bitcast(I32)
         )
         nc.sync.dma_start(line_sb[:], line)
-        x_scale_rows = sbuf([P, S], U8, "x_scale_rows")
+        x_scale_rows = sbuf(0, S, U8, "x_scale_rows")
         nc.vector.tensor_copy(x_scale_rows[:], x_scale_table[:].indirect(offs_sb[:]))
         for q in range(4):
             lo = P - SCALE_ROWS + 4 * q
@@ -73,14 +84,14 @@ def tile_picked_ydcons_relu_po_kernel(
             )
         w2_rows = w2.rearrange("(p j) c -> p j c", j=PACK)
         w2_cols = ((0, W2_FIRST), (W2_FIRST, N))
-        w2_halves = [placed_at(PACK * lo * 4, [P, PACK * (hi - lo)], F32, "w2_raw%d" % lo) for lo, hi in w2_cols]
+        w2_halves = [placed_at(w2_at + PACK * lo * 4, [P, PACK * (hi - lo)], F32, "w2_raw%d" % lo) for lo, hi in w2_cols]
         for raw, (lo, hi) in zip(w2_halves, w2_cols):
             nc.sync.dma_start(raw[:].rearrange("p (j c) -> p j c", j=PACK), w2_rows[:, :, lo:hi])
 
-        def quantize(values, name):
+        def quantize(values, stretch, name):
             width = values.shape[1] // PACK
-            codes = sbuf([P, width], U32, name + "_codes")
-            scales = sbuf([P, width], U8, name + "_scales")
+            codes = sbuf(stretch, width, U32, name + "_codes")
+            scales = sbuf(1, width, U8, name + "_scales")
             nc.vector.quantize_mx(out=codes[:].bitcast(FP8X4), scales=scales[:], in_=values)
             return codes, scales
 
@@ -95,22 +106,24 @@ def tile_picked_ydcons_relu_po_kernel(
                 stop=True,
             )
 
-        w1_bf16 = sbuf([P, PACK * H], BF16, "w1_bf16")
+        w1_bf16 = sbuf(2, PACK * H, BF16, "w1_bf16")
         dst = w1_bf16[:].rearrange("p (t m j) -> p m j t", t=PACK, j=PACK)
         src = w1_raw[:].rearrange("p j (m t) -> p m j t", t=PACK)
         nc.vector.tensor_copy(dst[:, :W1_VECTOR_M], src[:, :W1_VECTOR_M])
         nc.scalar.copy(dst[:, W1_VECTOR_M:], src[:, W1_VECTOR_M:])
-        w1_q = quantize(w1_bf16[:], "w1")
-        meas_raw = sbuf([P, PACK * V], F32, "meas_raw", "w1_raw")
+        w1_q = quantize(w1_bf16[:], 4, "w1")
+        meas_raw = placed_at(w1_at, [P, PACK * V], F32, "meas_raw")
         nc.sync.dma_start(meas_raw[:], meas.rearrange("(p t) v -> p (t v)", t=PACK))
 
         half = S // 2
-        x_picked = placed_at(PACK * N * 4, [P, S], U32, "x_picked")
+        x_picked = sbuf(2, S, U32, "x_picked")
         for lo, hi in ((0, CHUNK), (CHUNK, half), (half, S)):
             nc.vector.tensor_copy(x_picked[:, lo:hi], x_word_table[:].indirect(offs_sb[:, lo // 16 : hi // 16]))
 
         runs = ((0, CHUNK), (CHUNK, EARLY), (EARLY, S))
-        h_bf16 = [sbuf([P, (hi - lo) * PACK], BF16, "h_bf16_%d" % i) for i, (lo, hi) in enumerate(runs)]
+        h_bf16 = [sbuf(5, (hi - lo) * PACK, BF16, "h_bf16_%d" % lo) for lo, hi in runs[:2]]
+        h_last_at = reserve(5, PACK * V * 4)
+        h_bf16.append(placed_at(h_last_at, [P, CHUNK * PACK], BF16, "h_bf16_last"))
         for values, (lo, hi) in zip(h_bf16, runs):
             for first in range(lo, hi, CHUNK):
                 bank = ps.tile([P, PACK, CHUNK], F32, name="h_bank%d" % (first // CHUNK))
@@ -122,7 +135,7 @@ def tile_picked_ydcons_relu_po_kernel(
                     dst.rearrange("p (n t) -> p n t", t=PACK), bank[:].rearrange("p t n -> p n t"), ACT.Relu
                 )
 
-        w2_bf16 = sbuf([P, PACK * N], BF16, "w2_bf16")
+        w2_bf16 = sbuf(4, PACK * N, BF16, "w2_bf16")
         w2_dst = w2_bf16[:].rearrange("p (t m j) -> p m j t", t=PACK, j=PACK)
 
         def deal_w2(u, t_lo, t_hi):
@@ -136,11 +149,11 @@ def tile_picked_ydcons_relu_po_kernel(
         def quantize_h(i, offset):
             lo, hi = runs[i]
             codes = placed_at(offset, [P, hi - lo], U32, "h_codes%d" % i)
-            scales = sbuf([P, hi - lo], U8, "h_scales%d" % i)
+            scales = sbuf(1, hi - lo, U8, "h_scales%d" % i)
             nc.vector.quantize_mx(out=codes[:].bitcast(FP8X4), scales=scales[:], in_=h_bf16[i][:])
             h_q.append((codes, scales))
 
-        y_tiles = [sbuf([P, S], F32, "y%d" % t) for t in range(PACK)]
+        y_tiles = [sbuf(1 + t, S, F32, "y%d" % t) for t in range(PACK)]
 
         def second_layer(t, lo, hi, bank_tag, engine_copy):
             weights = w2_q[t // 2]
@@ -155,13 +168,13 @@ def tile_picked_ydcons_relu_po_kernel(
 
         deal_w2(0, 0, PACK)
         deal_w2(1, 0, PACK)
-        quantize_h(0, half_bytes + 4 * EARLY)
-        w2_q = [quantize(w2_bf16[:, : 2 * P * PACK], "w2_low")]
-        quantize_h(1, half_bytes)
-        quantize_h(2, half_bytes + 4 * half)
-        w2_q.append(quantize(w2_bf16[:, 2 * P * PACK :], "w2_high"))
+        quantize_h(0, w2_last_at + 4 * EARLY)
+        w2_q = [quantize(w2_bf16[:, : 2 * P * PACK], 6, "w2_low")]
+        quantize_h(1, w2_last_at)
+        quantize_h(2, w2_last_at + 4 * half)
+        w2_q.append(quantize(w2_bf16[:, 2 * P * PACK :], 6, "w2_high"))
 
-        meas3 = sbuf([P, PACK * V], F32, "meas3", "h_bf16_2")
+        meas3 = placed_at(h_last_at, [P, PACK * V], F32, "meas3")
         for u in range(2):
             cols = slice(2 * u * V, 2 * (u + 1) * V)
             nc.vector.tensor_scalar(meas3[:, cols], meas_raw[:, cols], 3.0, None, ALU.mult)
@@ -175,7 +188,7 @@ def tile_picked_ydcons_relu_po_kernel(
         second_layer(3, 0, half, "h_bank1", nc.vector.tensor_copy)
         second_layer(3, half, S, "y_bank0", nc.scalar.copy)
 
-        picked = [sbuf([P, V], F32, "picked%d" % t) for t in range(PACK)]
+        picked = [sbuf(6, V, F32, "picked%d" % t) for t in range(PACK)]
         for t in range(PACK):
             nc.vector.tensor_tensor(
                 picked[t][:], y_tiles[t][:].indirect(line_sb[:]), meas3[:, t * V : (t + 1) * V], ALU.add
@@ -197,7 +210,7 @@ def tile_picked_ydcons_relu_po_kernel(
         put_back(3, 0, V, True)
         put_back(2, SHARED, V, False)
 
-        pairs = sbuf([P, 2 * S * 2], BF16, "pairs", "h_bf16_2")
+        pairs = placed_at(h_last_at, [P, 2 * S * 2], BF16, "pairs")
 
         def round_rows(t, lo, hi, engine_copy):
             rows = pairs[:].rearrange("p (a n b) -> p a n b", a=2, b=2)
@@ -211,7 +224,7 @@ def tile_picked_ydcons_relu_po_kernel(
             round_rows(2, lo, hi, nc.vector.tensor_copy)
         round_rows(3, VECTOR_COLS, S, nc.scalar.copy)
         round_rows(2, VECTOR_COLS, S, nc.scalar.copy)
-        out_bf16 = [sbuf([P, (hi - lo) * PACK], BF16, "out_bf16_%d" % lo) for lo, hi in pieces]
+        out_bf16 = [sbuf(6, (hi - lo) * PACK, BF16, "out_bf16_%d" % lo) for lo, hi in pieces]
 
         def weave(i, engine_copy, dtype):
             lo, hi = pieces[i]
@@ -223,8 +236,8 @@ def tile_picked_ydcons_relu_po_kernel(
         weave(0, nc.vector.tensor_copy, I32)
         weave(1, nc.vector.tensor_copy, I32)
         weave(2, nc.scalar.copy, U32)
-        out_codes = sbuf([P, S], U32, "out_codes")
-        out_scales = sbuf([P, S], U8, "out_scales")
+        out_codes = sbuf(0, S, U32, "out_codes")
+        out_scales = sbuf(1, S, U8, "out_scales")
         out_words = out_1[0].rearrange("p n t -> p (n t)").bitcast(I32)
         for values, (lo, hi) in zip(out_bf16, pieces):
             nc.vector.quantize_mx(out=out_codes[:, lo:hi].bitcast(FP8X4), scales=out_scales[:, lo:hi], in_=values[:])

@@ -167,8 +167,9 @@ def tile_picked_ydcons_relu_po_kernel(
             engine_copy(y_tiles[t][:, lo:hi], bank[:, lo:hi])
 
         deal_w2(0, 0, PACK)
-        deal_w2(1, 0, PACK)
-        quantize_h(0, w2_last_at + 4 * EARLY)
+        quantize_h(0, w2_at)
+        deal_w2(1, 0, 2)
+        deal_w2(1, 2, PACK)
         w2_q = [quantize(w2_bf16[:, : 2 * P * PACK], 6, "w2_low")]
         quantize_h(1, w2_last_at)
         quantize_h(2, w2_last_at + 4 * half)

@@ -63,9 +63,9 @@ def tile_picked_ydcons_relu_po_kernel(
         x_scales_picked = sbuf(0, S, U8, "x_scales_picked")
         nc.gpsimd.memset(x_scales_picked[:].bitcast(I32), 0)
         ones = sbuf(0, V, F32, "ones")
-        nc.gpsimd.memset(ones[:], 1.0)
+        nc.gpsimd.memset(ones[:, : V // 2], 1.0)
         quarter = sbuf(0, V, F32, "quarter")
-        nc.scalar.mul(quarter[:], ones[:], 0.25)
+        nc.scalar.mul(quarter[:, : V // 2], ones[:, : V // 2], 0.25)
 
         w1_at = reserve(0, PACK * H * 4)
         w1_raw = placed_at(w1_at, [P, PACK, H], F32, "w1_raw")
@@ -79,9 +79,12 @@ def tile_picked_ydcons_relu_po_kernel(
         nc.vector.tensor_copy(x_scale_rows[:], x_scale_table[:].indirect(offs_sb[:]))
         for q in range(4):
             lo = P - SCALE_ROWS + 4 * q
-            nc.sync.dma_start(
+            nc.scalar.dma_start(
                 x_scales_picked[32 * q : 32 * q + 4, :].bitcast(I32), x_scale_rows[lo : lo + 4, :].bitcast(I32)
             )
+        late_ones = placed_at(w2_last_at - V, [P, V // 2], F32, "late_ones")
+        nc.gpsimd.memset(late_ones[:], 1.0)
+        nc.scalar.mul(quarter[:, V // 2 :], late_ones[:], 0.25)
         w2_rows = w2.rearrange("(p j) c -> p j c", j=PACK)
         w2_cols = ((0, W2_FIRST), (W2_FIRST, N))
         w2_halves = [placed_at(w2_at + PACK * lo * 4, [P, PACK * (hi - lo)], F32, "w2_raw%d" % lo) for lo, hi in w2_cols]

from contextlib import ExitStack

import concourse.mybir as mybir

K, T, S, H, N, V = 512, 2048, 512, 512, 512, 256
FLOPS = 2 * K * H * S + 2 * H * N * S

F32 = mybir.dt.float32
BF16 = mybir.dt.bfloat16
I32 = mybir.dt.int32
U32 = mybir.dt.uint32
U16 = mybir.dt.uint16
U8 = mybir.dt.uint8
FP8X4 = mybir.dt.float8_e4m3fn_x4
ALU = mybir.AluOpType
ACT = mybir.ActivationFunctionType

P = 128
PACK = 4
CHUNK = 128
EARLY = S - CHUNK
SCALE_ROWS = 16
W1_VECTOR_M = 84
VECTOR_COLS = 384
SHARED = 64
STRETCH = 32768
STRETCH_START = 1024
BYTES_OF = {F32: 4, U32: 4, BF16: 2, U8: 1}
W2_FIRST = 320


def tile_picked_ydcons_relu_po_kernel(
    tc, x_words, x_scales, w1, w2, meas, offs, line, out_0, out_1, out_2
):
    nc = tc.nc
    with ExitStack() as ctx:
        lists = ctx.enter_context(tc.tile_pool(name="lists", bufs=1))
        sb = ctx.enter_context(tc.tile_pool(name="sb", bufs=1))
        ps = ctx.enter_context(tc.psum_pool(name="ps", bufs=1))

        offs_sb = lists.tile([P, S // 16], U16, name="offs_sb")
        line_sb = lists.tile([P, V // 16], U16, name="line_sb")

        free = [r * STRETCH + STRETCH_START for r in range(7)]

        def reserve(stretch, size):
            at = free[stretch]
            free[stretch] = at + size
            return at

        def placed_at(offset, shape, dtype, name):
            return sb.tile(shape, dtype, name=name, align_bytes=64, offset=offset)

        def sbuf(stretch, columns, dtype, name):
            return placed_at(reserve(stretch, columns * BYTES_OF[dtype]), [P, columns], dtype, name)

        w2_at = reserve(3, PACK * N * 4)
        w2_last_at = w2_at + PACK * W2_FIRST * 4
        x_scale_table = placed_at(w2_last_at - T // 2, [P, T], U8, "x_scale_table")
        nc.scalar.dma_start(x_scale_table[P - SCALE_ROWS :, :].bitcast(I32), x_scales[0].bitcast(I32))
        nc.sync.dma_start(offs_sb[:], offs)
        nc.gpsimd.memset(x_scale_table[: P - SCALE_ROWS, :].bitcast(I32), 0)
        x_scales_picked = sbuf(0, S, U8, "x_scales_picked")
        nc.gpsimd.memset(x_scales_picked[:].bitcast(I32), 0)
        ones = sbuf(0, V, F32, "ones")
        nc.gpsimd.memset(ones[:, : V // 2], 1.0)
        quarter = sbuf(0, V, F32, "quarter")
        nc.scalar.mul(quarter[:, : V // 2], ones[:, : V // 2], 0.25)

        w1_at = reserve(0, PACK * H * 4)
        w1_raw = placed_at(w1_at, [P, PACK, H], F32, "w1_raw")
        nc.sync.dma_start(w1_raw[:], w1.rearrange("(p j) c -> p j c", j=PACK))
        x_word_table = sbuf(1, T, U32, "x_word_table")
        nc.sync.dma_start(
            x_word_table[:].bitcast(I32), x_words[0].rearrange("p n t -> p (n t)").bitcast(I32)
        )
        nc.sync.dma_start(line_sb[:], line)
        x_scale_rows = sbuf(0, S, U8, "x_scale_rows")
        nc.vector.tensor_copy(x_scale_rows[:], x_scale_table[:].indirect(offs_sb[:]))
        for q in range(4):
            lo = P - SCALE_ROWS + 4 * q
            nc.scalar.dma_start(
                x_scales_picked[32 * q : 32 * q + 4, :].bitcast(I32), x_scale_rows[lo : lo + 4, :].bitcast(I32)
            )
        late_ones = placed_at(w2_last_at - V, [P, V // 2], F32, "late_ones")
        nc.gpsimd.memset(late_ones[:], 1.0)
        nc.scalar.mul(quarter[:, V // 2 :], late_ones[:], 0.25)
        w2_rows = w2.rearrange("(p j) c -> p j c", j=PACK)
        w2_cols = ((0, W2_FIRST), (W2_FIRST, N))
        w2_halves = [placed_at(w2_at + PACK * lo * 4, [P, PACK * (hi - lo)], F32, "w2_raw%d" % lo) for lo, hi in w2_cols]
        for raw, (lo, hi) in zip(w2_halves, w2_cols):
            nc.sync.dma_start(raw[:].rearrange("p (j c) -> p j c", j=PACK), w2_rows[:, :, lo:hi])

        def quantize(values, stretch, name):
            width = values.shape[1] // PACK
            codes = sbuf(stretch, width, U32, name + "_codes")
            scales = sbuf(1, width, U8, name + "_scales")
            nc.vector.quantize_mx(out=codes[:].bitcast(FP8X4), scales=scales[:], in_=values)
            return codes, scales

        def product(out, weights, w_cols, moving_codes, moving_scales):
            nc.tensor.matmul_mx(
                out=out,
                lhsT=weights[0][:, w_cols].bitcast(FP8X4),
                lhsT_scale=weights[1][:, w_cols],
                rhs=moving_codes.bitcast(FP8X4),
                rhs_scale=moving_scales,
                start=True,
                stop=True,
            )

        w1_bf16 = sbuf(2, PACK * H, BF16, "w1_bf16")
        dst = w1_bf16[:].rearrange("p (t m j) -> p m j t", t=PACK, j=PACK)
        src = w1_raw[:].rearrange("p j (m t) -> p m j t", t=PACK)
        nc.vector.tensor_copy(dst[:, :W1_VECTOR_M], src[:, :W1_VECTOR_M])
        nc.scalar.copy(dst[:, W1_VECTOR_M:], src[:, W1_VECTOR_M:])
        w1_q = quantize(w1_bf16[:], 4, "w1")
        meas_raw = placed_at(w1_at, [P, PACK * V], F32, "meas_raw")
        nc.sync.dma_start(meas_raw[:], meas.rearrange("(p t) v -> p (t v)", t=PACK))

        half = S // 2
        x_picked = sbuf(2, S, U32, "x_picked")
        for lo, hi in ((0, CHUNK), (CHUNK, half), (half, S)):
            nc.vector.tensor_copy(x_picked[:, lo:hi], x_word_table[:].indirect(offs_sb[:, lo // 16 : hi // 16]))

        runs = ((0, CHUNK), (CHUNK, EARLY), (EARLY, S))
        h_bf16 = [sbuf(5, (hi - lo) * PACK, BF16, "h_bf16_%d" % lo) for lo, hi in runs[:2]]
        h_last_at = reserve(5, PACK * V * 4)
        h_bf16.append(placed_at(h_last_at, [P, CHUNK * PACK], BF16, "h_bf16_last"))
        for values, (lo, hi) in zip(h_bf16, runs):
            for first in range(lo, hi, CHUNK):
                bank = ps.tile([P, PACK, CHUNK], F32, name="h_bank%d" % (first // CHUNK))
                cols = slice(first, first + CHUNK)
                for t in range(PACK):
                    product(bank[:, t, :], w1_q, slice(t * P, (t + 1) * P), x_picked[:, cols], x_scales_picked[:, cols])
                dst = values[:, (first - lo) * PACK : (first - lo + CHUNK) * PACK]
                nc.scalar.activation(
                    dst.rearrange("p (n t) -> p n t", t=PACK), bank[:].rearrange("p t n -> p n t"), ACT.Relu
                )

        w2_bf16 = sbuf(4, PACK * N, BF16, "w2_bf16")
        w2_dst = w2_bf16[:].rearrange("p (t m j) -> p m j t", t=PACK, j=PACK)

        def deal_w2(u, t_lo, t_hi):
            src = w2_halves[u][:].rearrange("p (j m t) -> p m j t", j=PACK, t=PACK)
            nc.vector.tensor_copy(
                w2_dst[:, w2_cols[u][0] // PACK : w2_cols[u][1] // PACK, :, t_lo:t_hi], src[:, :, :, t_lo:t_hi]
            )

        h_q = []

        def quantize_h(i, offset):
            lo, hi = runs[i]
            codes = placed_at(offset, [P, hi - lo], U32, "h_codes%d" % i)
            scales = sbuf(1, hi - lo, U8, "h_scales%d" % i)
            nc.vector.quantize_mx(out=codes[:].bitcast(FP8X4), scales=scales[:], in_=h_bf16[i][:])
            h_q.append((codes, scales))

        y_tiles = [sbuf(1 + t, S, F32, "y%d" % t) for t in range(PACK)]

        def second_layer(t, lo, hi, bank_tag, engine_copy):
            weights = w2_q[t // 2]
            w_cols = slice(t % 2 * P, (t % 2 + 1) * P)
            bank = ps.tile([P, S], F32, name="y_bank%d_%d" % (t, lo), tag=bank_tag)
            for (codes, scales), (first, last) in zip(h_q, runs):
                a, b = max(lo, first), min(hi, last)
                if a < b:
                    part = slice(a - first, b - first)
                    product(bank[:, a:b], weights, w_cols, codes[:, part], scales[:, part])
            engine_copy(y_tiles[t][:, lo:hi], bank[:, lo:hi])

        deal_w2(0, 0, PACK)
        quantize_h(0, w2_at)
        deal_w2(1, 0, 2)
        deal_w2(1, 2, PACK)
        w2_q = [quantize(w2_bf16[:, : 2 * P * PACK], 6, "w2_low")]
        quantize_h(1, w2_last_at)
        quantize_h(2, w2_last_at + 4 * half)
        w2_q.append(quantize(w2_bf16[:, 2 * P * PACK :], 6, "w2_high"))

        meas3 = placed_at(h_last_at, [P, PACK * V], F32, "meas3")
        for u in range(2):
            cols = slice(2 * u * V, 2 * (u + 1) * V)
            nc.vector.tensor_scalar(meas3[:, cols], meas_raw[:, cols], 3.0, None, ALU.mult)

        second_layer(0, 0, CHUNK, "y_bank0", nc.scalar.copy)
        second_layer(1, 0, CHUNK, "y_bank1", nc.scalar.copy)
        second_layer(0, CHUNK, EARLY, "h_bank0", nc.scalar.copy)
        second_layer(0, EARLY, S, "h_bank1", nc.scalar.copy)
        second_layer(1, CHUNK, S, "h_bank2", nc.scalar.copy)
        second_layer(2, 0, S, "y_bank2", nc.scalar.copy)
        second_layer(3, 0, half, "h_bank1", nc.vector.tensor_copy)
        second_layer(3, half, S, "y_bank0", nc.scalar.copy)

        picked = [sbuf(6, V, F32, "picked%d" % t) for t in range(PACK)]
        for t in range(PACK):
            nc.vector.tensor_tensor(
                picked[t][:], y_tiles[t][:].indirect(line_sb[:]), meas3[:, t * V : (t + 1) * V], ALU.add
            )
        out_rows = out_0.rearrange("(p t) n -> p t n", t=PACK)

        def put_back(t, lo, hi, on_vector):
            target = y_tiles[t][:].indirect(line_sb[:, lo // 16 : hi // 16])
            if on_vector:
                nc.vector.tensor_tensor(target, picked[t][:, lo:hi], quarter[:, lo:hi], ALU.mult)
            else:
                nc.scalar.activation(target, picked[t][:, lo:hi], ACT.Copy, scale=0.25)
            if hi == V:
                nc.sync.dma_start(out_rows[:, t, :], y_tiles[t][:])

        put_back(0, 0, V, False)
        put_back(1, 0, V, False)
        put_back(2, 0, SHARED, True)
        put_back(3, 0, V, True)
        put_back(2, SHARED, V, False)

        pairs = placed_at(h_last_at, [P, 2 * S * 2], BF16, "pairs")

        def round_rows(t, lo, hi, engine_copy):
            rows = pairs[:].rearrange("p (a n b) -> p a n b", a=2, b=2)
            engine_copy(rows[:, t // 2, lo:hi, t % 2], y_tiles[t][:, lo:hi])

        round_rows(0, 0, S, nc.vector.tensor_copy)
        round_rows(1, 0, S, nc.vector.tensor_copy)
        round_rows(3, 0, VECTOR_COLS, nc.vector.tensor_copy)
        pieces = ((0, CHUNK), (CHUNK, VECTOR_COLS), (VECTOR_COLS, S))
        for lo, hi in pieces[:2]:
            round_rows(2, lo, hi, nc.vector.tensor_copy)
        round_rows(3, VECTOR_COLS, S, nc.scalar.copy)
        round_rows(2, VECTOR_COLS, S, nc.scalar.copy)
        out_bf16 = [sbuf(6, (hi - lo) * PACK, BF16, "out_bf16_%d" % lo) for lo, hi in pieces]

        def weave(i, engine_copy, dtype):
            lo, hi = pieces[i]
            engine_copy(
                out_bf16[i][:].bitcast(dtype).rearrange("p (n a) -> p n a", a=2),
                pairs[:].bitcast(dtype).rearrange("p (a n) -> p n a", a=2)[:, lo:hi],
            )

        weave(0, nc.vector.tensor_copy, I32)
        weave(1, nc.vector.tensor_copy, I32)
        weave(2, nc.scalar.copy, U32)
        out_codes = sbuf(0, S, U32, "out_codes")
        out_scales = sbuf(1, S, U8, "out_scales")
        out_words = out_1[0].rearrange("p n t -> p (n t)").bitcast(I32)
        for values, (lo, hi) in zip(out_bf16, pieces):
            nc.vector.quantize_mx(out=out_codes[:, lo:hi].bitcast(FP8X4), scales=out_scales[:, lo:hi], in_=values[:])
            nc.sync.dma_start(out_words[:, lo:hi], out_codes[:, lo:hi].bitcast(I32))
        for q in range(4):
            queue = nc.scalar if q < 2 else nc.sync
            queue.dma_start(
                out_2[0, 4 * q : 4 * q + 4, :].bitcast(I32),
                out_scales[32 * q : 32 * q + 4, :].bitcast(I32),
            )
